import numpy as np
import ml_dtypes


def mxq(x, axis, fmt="e4m3"):
    dtype, down = {"e4m3": (ml_dtypes.float8_e4m3fn, 7), "e5m2": (ml_dtypes.float8_e5m2, 14)}[fmt]
    v = np.moveaxis(np.asarray(x, np.float32).astype(ml_dtypes.bfloat16).astype(np.float64), axis, -1)
    blocks = v.reshape(v.shape[:-1] + (-1, 32))
    amax = np.abs(blocks).max(-1, keepdims=True)
    byte = np.maximum(np.where(amax > 0, np.frexp(amax)[1] - 1 + 127, 0) - down, 1)
    scale = np.exp2(byte - 127.0)
    codes = (blocks / scale).astype(np.float32).astype(dtype).astype(np.float64)
    return np.moveaxis((codes * scale).reshape(v.shape), -1, axis)


WIDE = False


def mx_kscale(k):
    if not WIDE:
        return np.ones(k)
    levels = np.array([10, -10, 5, -5, 0])
    if k % 512:
        return np.exp2(np.random.permutation(np.resize(levels, k // 32))).repeat(32)
    a = np.empty((k // 512, 16))
    for p in range(k // 512):
        a[p, :8] = np.random.permutation(np.resize(levels, 8))
        for g in range(8):
            far = levels[np.abs(levels - a[p, g]) >= 10]
            a[p, g + 8] = far[np.random.randint(len(far))]
    return np.exp2(a.ravel()).repeat(32)


def f64(x):
    return np.asarray(x).astype(np.float64)


def striped(idx):
    return np.tile(idx.reshape(-1, 16).T, (8, 1)).astype(np.uint16)


def unstriped(offs):
    return offs[:16].T.reshape(-1).astype(np.int64)


E2M1 = np.array([0.0, 0.5, 1.0, 1.5, 2.0, 3.0, 4.0, 6.0, -0.0, -0.5, -1.0, -1.5, -2.0, -3.0, -4.0, -6.0])


def pack_weight(w, fmt):
    k, n = w.shape
    w = f64(np.asarray(w, np.float32).astype(ml_dtypes.bfloat16)).reshape(k // 32, 32, n)
    amax = np.abs(w).max(1)
    if fmt == "e4m3":
        byte = np.frexp(amax)[1] - 1 + 127 - 7
    else:
        mant, ex = np.frexp(amax / 6.0)
        byte = np.where(mant > 0.5, ex, ex - 1) + 127
    byte = np.clip(np.where(amax > 0, byte, 1), 1, 254)
    scaled = (w * np.exp2(127.0 - byte)[:, None, :]).reshape(k, n).astype(np.float32)
    by_word = np.ascontiguousarray(scaled.reshape(k // 512, 128, 4, n).transpose(0, 1, 3, 2))
    if fmt == "e4m3":
        words = by_word.astype(ml_dtypes.float8_e4m3fn).view(np.uint8)
    else:
        c = by_word.astype(ml_dtypes.float4_e2m1fn).view(np.uint8) & 0xF
        words = (c[..., 0::2] | (c[..., 1::2] << 4)).reshape(k // 512, 128, 2 * n)
    return np.ascontiguousarray(words), np.ascontiguousarray(byte.astype(np.uint8).reshape(k // 512, 16, n))


def unpack_weight(words, scales, fmt):
    g, _, n = scales.shape
    words = np.ascontiguousarray(words).reshape(g, 128, n, -1)
    if fmt == "e4m3":
        vals = words.view(ml_dtypes.float8_e4m3fn).astype(np.float64)
    else:
        nib = np.empty((g, 128, n, 4), np.uint8)
        nib[..., 0::2] = words & 0xF
        nib[..., 1::2] = words >> 4
        vals = E2M1[nib]
    vals = vals * np.repeat(np.exp2(scales.astype(np.float64) - 127.0), 8, axis=1)[..., None]
    return vals.transpose(0, 1, 3, 2).reshape(g * 512, n)


def gelu(v):
    return 0.5 * v * (1.0 + np.tanh(np.sqrt(2.0 / np.pi) * (v + 0.044715 * v**3)))


K, T, E, C, H, N = 1024, 768, 6, 256, 512, 128


def by_expert(wq, xq):
    return np.concatenate([wq[e].T @ xq[:, e * C:(e + 1) * C] for e in range(E)], axis=1)


def setup_inputs():
    n = np.random.standard_normal
    s = mx_kscale(K)[:, None]
    u = mx_kscale(H)
    first = np.random.permutation(np.repeat(np.arange(E), T // E))
    second = (first + 1 + np.random.permutation(np.repeat(np.arange(E - 1), -(-T // (E - 1)))[:T])) % E
    while np.bincount(second, minlength=E).max() != T // E:
        load = np.bincount(second, minlength=E); hi, lo = int(load.argmax()), int(load.argmin())
        t = np.flatnonzero((second == hi) & (first != lo))[0]; second[t] = lo
    slot_token = np.empty(E * C, np.int64); pos = np.empty((2, T), np.int64); fill = np.zeros(E, np.int64)
    place = np.stack([np.random.permutation(C) for _ in range(E)])
    for r, deal in enumerate((first, second)):
        for t in np.random.permutation(T):
            e = deal[t]; j = e * C + place[e, fill[e]]; fill[e] += 1; slot_token[j] = t; pos[r, t] = j
    g = np.random.uniform(0.2, 0.8, T)
    w1 = [pack_weight(m, "e2m1") for m in n((E + 1, K, H)) / np.sqrt(K) / s[None]]
    w3 = [pack_weight(m, "e2m1") for m in n((E + 1, K, H)) / np.sqrt(K) / s[None] * u[None, None, :]]
    w2 = [pack_weight(m, "e2m1") for m in n((E + 1, H, N)) / np.sqrt(H) / u[None, :, None]]
    x = pack_weight(n((K, T)) * s, "e4m3")
    return {
        "x_words": x[0],
        "x_scales": x[1],
        "w1_words": np.stack([m[0] for m in w1]),
        "w1_scales": np.stack([m[1] for m in w1]),
        "w3_words": np.stack([m[0] for m in w3]),
        "w3_scales": np.stack([m[1] for m in w3]),
        "w2_words": np.stack([m[0] for m in w2]),
        "w2_scales": np.stack([m[1] for m in w2]),
        "gate": np.stack([np.tile(g, (N, 1)), np.tile(1.0 - g, (N, 1))]).astype(np.float32),
        "offs": striped(slot_token),
        "pos1": striped(pos[0]),
        "pos2": striped(pos[1]),
    }


def reference(x_words, x_scales, w1_words, w1_scales, w3_words, w3_scales, w2_words, w2_scales, gate, offs, pos1, pos2):
    idx = unstriped(offs)
    w1 = np.stack([unpack_weight(w1_words[e], w1_scales[e], "e2m1") for e in range(E + 1)])
    w3 = np.stack([unpack_weight(w3_words[e], w3_scales[e], "e2m1") for e in range(E + 1)])
    w2 = np.stack([unpack_weight(w2_words[e], w2_scales[e], "e2m1") for e in range(E + 1)])
    w1q, w3q, w2q = w1, w3, w2
    xs = unpack_weight(x_words, x_scales, "e4m3")
    hs = gelu(w1q[E].T @ xs) * (w3q[E].T @ xs)
    ys = w2q[E].T @ mxq(hs, 0, "e4m3")
    xq = unpack_weight(x_words, x_scales, "e4m3")[:, idx]
    h = gelu(by_expert(w1q, xq))
    h = h * by_expert(w3q, xq)
    y = by_expert(w2q, mxq(h, 0, "e4m3"))
    return ys + f64(gate[0]) * y[:, unstriped(pos1)] + f64(gate[1]) * y[:, unstriped(pos2)]

@@ -1,0 +1,265 @@
+from contextlib import ExitStack
+
+import concourse.mybir as mybir
+from concourse.masks import make_identity
+
+K, T, E, C, H, N = 1024, 768, 6, 256, 512, 128
+P = 128
+PASSES = 2
+S = E * C
+FLOPS = 2 * (S + T) * (2 * K * H + H * N)
+
+F32 = mybir.dt.float32
+BF16 = mybir.dt.bfloat16
+I32 = mybir.dt.int32
+U32 = mybir.dt.uint32
+U16 = mybir.dt.uint16
+U8 = mybir.dt.uint8
+FP8X4 = mybir.dt.float8_e4m3fn_x4
+FP4X4 = mybir.dt.float4_e2m1fn_x4
+GELU = mybir.ActivationFunctionType.Gelu_apprx_tanh
+MULT = mybir.AluOpType.mult
+ADD = mybir.AluOpType.add
+
+
+def tile_moe_shr_glu_gelu_kernel(
+    tc, x_words, x_scales, w1_words, w1_scales, w3_words, w3_scales, w2_words, w2_scales, gate, offs, pos1, pos2, out
+):
+    nc = tc.nc
+    with ExitStack() as ctx:
+        keep = ctx.enter_context(tc.tile_pool(name="keep", bufs=1))
+        ring = ctx.enter_context(tc.tile_pool(name="ring", bufs=2))
+        psum = ctx.enter_context(tc.psum_pool(name="psum", bufs=1))
+
+        def plane(name, width):
+            t = keep.tile([P, width], U8, name=name, align_bytes=64)
+            nc.vector.memset(t[:].bitcast(I32), 0)
+            return t
+
+        def load_scales(queue, t, rows):
+            src = rows.bitcast(I32).rearrange("g (q r) c -> r q g c", r=4)
+            dst = t[:].bitcast(I32).rearrange("p (g c) -> p g c", g=rows.shape[0])
+            for r in range(4):
+                queue.dma_start(out=dst[r:P:32], in_=src[r])
+
+        def load_words(name, words, e):
+            t = ring.tile([P, PASSES, 2 * H], U8, name=name, tag=name, bufs=6, align_bytes=64)
+            nc.sync.dma_start(out=t[:].bitcast(I32), in_=words[e].bitcast(I32).rearrange("s p c -> p s c"))
+            return t
+
+        def shared_words(name, words):
+            t = keep.tile([P, PASSES, 2 * H], U8, name=name, align_bytes=64)
+            nc.sync.dma_start(out=t[:].bitcast(I32), in_=words[E].bitcast(I32).rearrange("s p c -> p s c"))
+            return t
+
+        xs = plane("xs", PASSES * T)
+        FIRST = E - 1
+        s1a = plane("s1a", 2 * PASSES * H)
+        s3a = plane("s3a", 2 * PASSES * H)
+        xp = plane("xp", T)
+        s2 = plane("s2", (E + 1) * N)
+        s1b = plane("s1b", FIRST * PASSES * H)
+        s3b = plane("s3b", FIRST * PASSES * H)
+
+        offs_sb = keep.tile([P, S // 16], U16, name="offs_sb")
+        nc.sync.dma_start(offs_sb[:], offs)
+        xw = [keep.tile([P, T], U32, name="xw%d" % o, align_bytes=64) for o in range(PASSES)]
+        nc.sync.dma_start(out=xw[0][:].bitcast(I32), in_=x_words[0].rearrange("p t r -> p (t r)").bitcast(I32))
+        load_scales(nc.sync, xs, x_scales)
+        w1s = shared_words("w1s", w1_words)
+        nc.sync.dma_start(out=xw[1][:].bitcast(I32), in_=x_words[1].rearrange("p t r -> p (t r)").bitcast(I32))
+        load_scales(nc.sync, s1a, w1_scales[FIRST:].rearrange("e s q c -> (e s) q c"))
+        w3s = shared_words("w3s", w3_words)
+        load_scales(nc.sync, s3a, w3_scales[FIRST:].rearrange("e s q c -> (e s) q c"))
+        ident = keep.tile([P, P], F32, name="ident")
+        make_identity(nc, ident[:])
+
+        y = keep.tile([P, S], F32, name="y")
+        w2 = keep.tile([P, E + 1, 2 * N], U8, name="w2", align_bytes=64)
+        ys0 = keep.tile([P, C], F32, name="ys0")
+
+        def gather_bytes_apart(first):
+            tiles = []
+            for o in range(PASSES):
+                g = keep.tile([P, 2 * C], U8, name="ga%d" % o, align_bytes=64)
+                nc.vector.tensor_copy(g[:], xs[:, o * T : (o + 1) * T].indirect(offs_sb[:, first * 16 : (first + 2) * 16]))
+                tiles.append(g)
+            return tiles
+
+        def gather_bytes(first):
+            g = ring.tile([P, 2 * C], U8, name="gb", tag="gb", bufs=2, align_bytes=64)
+            nc.vector.tensor_copy(g[:], xp[:].indirect(offs_sb[:, first * 16 : (first + 2) * 16]))
+            m = ring.tile([P, 2 * C], U8, name="mb", tag="mb", bufs=2, align_bytes=64)
+            nc.gpsimd.dma_start(out=m[0:64, :].bitcast(I32), in_=g[4:68, :].bitcast(I32))
+            nc.gpsimd.dma_start(out=m[64:128, :].bitcast(I32), in_=g[8:72, :].bitcast(I32))
+            return g, m
+
+        def gather_words(e):
+            tiles = []
+            for o in range(PASSES):
+                g = ring.tile([P, C], U32, name="gw%d" % o, tag="gw%d" % o, bufs=2, align_bytes=64)
+                nc.vector.tensor_copy(g[:], xw[o][:].indirect(offs_sb[:, e * 16 : (e + 1) * 16]))
+                tiles.append(g)
+            return tiles
+
+        def first_layer(words, scales, w1, w3, sc1, sc3):
+            hs = []
+            for j in range(2):
+                cols = slice(j * P, (j + 1) * P)
+                a = psum.tile([P, H], F32, name="a", tag="a", bufs=2)
+                b = psum.tile([P, H], F32, name="b", tag="b", bufs=3)
+                for acc, w, sc in ((a, w1, sc1), (b, w3, sc3)):
+                    for o in range(PASSES):
+                        nc.tensor.matmul_mx(
+                            out=acc[:],
+                            lhsT=words[o][:, cols].bitcast(FP8X4),
+                            lhsT_scale=scales[o][:, cols],
+                            rhs=w[:, o, :].bitcast(FP4X4),
+                            rhs_scale=sc[:, o * H : (o + 1) * H],
+                            start=(o == 0),
+                            stop=(o == PASSES - 1),
+                        )
+                g = ring.tile([P, H], F32, name="g", tag="g", bufs=3)
+                nc.scalar.activation(
+                    out=g[:].rearrange("q (u p e) -> q u p e", u=2, e=2),
+                    in_=a[:].rearrange("q (p u e) -> q u p e", u=2, e=2),
+                    func=GELU,
+                )
+                h = ring.tile([P, H], BF16, name="h", tag="h", bufs=4, align_bytes=64)
+                nc.vector.tensor_tensor(
+                    out=h[:].rearrange("q (u p e) -> q u p e", u=2, e=2),
+                    in0=b[:].rearrange("q (p u e) -> q u p e", u=2, e=2),
+                    in1=g[:].rearrange("q (u p e) -> q u p e", u=2, e=2),
+                    op=MULT,
+                )
+                hs.append(h)
+            return hs
+
+        def turn_and_quantise(hs):
+            tr = psum.tile([P, 4, P], F32, name="tr", tag="tr", bufs=1)
+            for j in range(2):
+                for u in range(2):
+                    nc.tensor.transpose(tr[:, 2 * j + u, :], hs[j][:].bitcast(F32)[:, u * P : (u + 1) * P], ident[:])
+            ht = ring.tile([P, 4 * C], BF16, name="ht", tag="ht", bufs=2, align_bytes=64)
+            nc.scalar.copy(
+                out=ht[:].bitcast(F32).rearrange("p (j s u) -> p j s u", j=2, u=2),
+                in_=tr[:].rearrange("p (j u) s -> p j s u", u=2),
+            )
+            hq = ring.tile([P, C], U32, name="hq", tag="hq", bufs=2, align_bytes=64)
+            hz = ring.tile([P, C], U8, name="hz", tag="hz", bufs=2, align_bytes=64)
+            nc.vector.quantize_mx(out=hq[:].bitcast(FP8X4), scales=hz[:], in_=ht[:])
+            return hq, hz
+
+        def second_layer(e, hq, hz):
+            acc = psum.tile([P, C], F32, name="yacc", tag="yacc", bufs=2)
+            nc.tensor.matmul_mx(
+                out=acc[:],
+                lhsT=w2[:, e, :].bitcast(FP4X4),
+                lhsT_scale=s2[:, e * N : (e + 1) * N],
+                rhs=hq[:].bitcast(FP8X4),
+                rhs_scale=hz[:],
+                start=True,
+                stop=True,
+            )
+            return acc
+
+        units = [("s", 0)] + [("e", e) for e in reversed(range(E))] + [("s", 1), ("s", 2)]
+        routed = [i for kind, i in units if kind == "e"]
+        weights = {}
+        tokens = {}
+        planes = {}
+
+        def prepare(e):
+            weights[e] = (load_words("w1", w1_words, e), load_words("w3", w3_words, e))
+            tokens[e] = gather_words(e)
+            if e == E - 1:
+                planes[e // 2] = gather_bytes_apart(e - 1)
+            elif e % 2 == 0 and e > 0:
+                planes[e // 2 - 1] = gather_bytes(e - 2)
+
+        prepare(routed[0])
+        load_scales(nc.sync, xp, x_scales[0:1])
+        SECOND = (4, 36, 8, 40)
+        for q in range(4):
+            nc.gpsimd.dma_start(
+                out=xp[SECOND[q] : SECOND[q] + 4, :].bitcast(I32), in_=x_scales[1, 4 * q : 4 * q + 4, :].bitcast(I32)
+            )
+        nc.sync.dma_start(out=w2[:].bitcast(I32), in_=w2_words.bitcast(I32).rearrange("e s p c -> p (e s) c"))
+        load_scales(nc.sync, s2, w2_scales.rearrange("e s q c -> (e s) q c"))
+        load_scales(nc.sync, s1b, w1_scales[:FIRST].rearrange("e s q c -> (e s) q c"))
+        load_scales(nc.sync, s3b, w3_scales[:FIRST].rearrange("e s q c -> (e s) q c"))
+        prepare(routed[1])
+        pos_sb = []
+        for name, pos in (("pos1_sb", pos1), ("pos2_sb", pos2)):
+            t = keep.tile([P, T // 16], U16, name=name)
+            nc.sync.dma_start(t[:], pos)
+            pos_sb.append(t)
+        gate_sb = keep.tile([P, 2, T], F32, name="gate_sb")
+
+        shared_sums = {}
+        hidden = {}
+        quantised = {}
+
+        def stage1(n):
+            kind, i = units[n]
+            if kind == "s":
+                cols = slice(i * C, (i + 1) * C)
+                words = [xw[o][:, cols] for o in range(PASSES)]
+                scales = [xs[:, o * T + i * C : o * T + (i + 1) * C] for o in range(PASSES)]
+                hidden[n] = first_layer(words, scales, w1s, w3s, s1a[:, PASSES * H :], s3a[:, PASSES * H :])
+            else:
+                cols = slice((i % 2) * C, (i % 2 + 1) * C)
+                scales = [t[:, cols] for t in planes[i // 2]]
+                if i >= FIRST:
+                    sc = [t[:, : PASSES * H] for t in (s1a, s3a)]
+                else:
+                    sc = [t[:, i * PASSES * H : (i + 1) * PASSES * H] for t in (s1b, s3b)]
+                hidden[n] = first_layer(tokens[i], scales, weights[i][0], weights[i][1], sc[0], sc[1])
+                nxt = routed.index(i) + 2
+                if nxt < E:
+                    prepare(routed[nxt])
+                if nxt == E:
+                    nc.sync.dma_start(out=gate_sb[:], in_=gate.rearrange("j p t -> p j t"))
+
+        def stage3(n):
+            kind, i = units[n]
+            acc = second_layer(E if kind == "s" else i, *quantised[n])
+            if kind == "e":
+                nc.scalar.copy(out=y[:, i * C : (i + 1) * C], in_=acc[:])
+            elif i == 0:
+                nc.scalar.copy(out=ys0[:], in_=acc[:])
+                shared_sums[i] = ys0
+            else:
+                shared_sums[i] = acc
+
+        last_routed = units.index(("e", routed[-1]))
+        steps = []
+        for n in range(len(units) + 2):
+            steps.extend([(1, n), (3, n - 2), (2, n - 1)])
+            if n == last_routed:
+                steps.extend([(3, n - 1), (2, n), (3, n)])
+        taken = set()
+        for stage, n in steps:
+            if 0 <= n < len(units) and (stage, n) not in taken:
+                taken.add((stage, n))
+                if stage == 1:
+                    stage1(n)
+                elif stage == 2:
+                    quantised[n] = turn_and_quantise(hidden[n])
+                else:
+                    stage3(n)
+
+        for c in range(T // C):
+            cols = slice(c * C, (c + 1) * C)
+            parts = []
+            for j in range(2):
+                t = ring.tile([P, C], F32, name="part%d" % j, tag="part%d" % j, bufs=3)
+                nc.vector.tensor_tensor(
+                    out=t[:], in0=y[:].indirect(pos_sb[j][:, c * 16 : (c + 1) * 16]), in1=gate_sb[:, j, cols], op=MULT
+                )
+                parts.append(t)
+            s = ring.tile([P, C], F32, name="s", tag="s", bufs=3)
+            nc.vector.tensor_tensor(out=s[:], in0=parts[0][:], in1=parts[1][:], op=ADD)
+            r = ring.tile([P, C], F32, name="r", tag="r", bufs=3)
+            nc.vector.tensor_tensor(out=r[:], in0=shared_sums[c][:], in1=s[:], op=ADD)
+            nc.sync.dma_start(out=out[:, cols], in_=r[:])

@@ -20,6 +20,11 @@ FP4X4 = mybir.dt.float4_e2m1fn_x4
 GELU = mybir.ActivationFunctionType.Gelu_apprx_tanh
 MULT = mybir.AluOpType.mult
 ADD = mybir.AluOpType.add
+FIRST = E - 1
+GATES = {("W", 2): 0, ("B", 2): 2, ("W", 1): 3, ("B", 1): 4, ("W", 0): 6, ("B", 0): 7}
+PLAN = [[1,0],[1,1],[1,2],[2,0,"A1"],[1,3],[2,1,"A0"],[1,4],[2,2,"A2"],[3,0,"A0"],[1,5],[2,3,"A1"],[3,1,"A2"],[1,6,0],[2,4,"y"],[3,2,"A0"],[1,6,1],[2,5,"y"],[3,3,"A1"],[1,7,0],[2,6,"y"],[3,4,"A2"],[3,5,"A1"],[1,7,1],[3,6,"y"],[1,8,0],[2,7,"A0"],[1,8,1],[2,8,"A1"],[3,7,"b"],[3,8,"b"]]
+UNITS = [("s", 0)] + [("e", e) for e in reversed(range(E))] + [("s", 1), ("s", 2)]
+COPIED = (0,)
 
 
 def tile_moe_shr_glu_gelu_kernel(
@@ -28,130 +33,157 @@ def tile_moe_shr_glu_gelu_kernel(
     nc = tc.nc
     with ExitStack() as ctx:
         keep = ctx.enter_context(tc.tile_pool(name="keep", bufs=1))
-        ring = ctx.enter_context(tc.tile_pool(name="ring", bufs=2))
+        work = ctx.enter_context(tc.tile_pool(name="work", bufs=1))
         psum = ctx.enter_context(tc.psum_pool(name="psum", bufs=1))
 
-        def plane(name, width):
+        def plane(name, width, engine):
             t = keep.tile([P, width], U8, name=name, align_bytes=64)
-            nc.vector.memset(t[:].bitcast(I32), 0)
+            engine.memset(t[:].bitcast(I32), 0)
             return t
 
-        def load_scales(queue, t, rows):
+        def load_scales(queue, t, rows, which=range(4)):
             src = rows.bitcast(I32).rearrange("g (q r) c -> r q g c", r=4)
             dst = t[:].bitcast(I32).rearrange("p (g c) -> p g c", g=rows.shape[0])
-            for r in range(4):
+            for r in which:
                 queue.dma_start(out=dst[r:P:32], in_=src[r])
 
-        def load_words(name, words, e):
-            t = ring.tile([P, PASSES, 2 * H], U8, name=name, tag=name, bufs=6, align_bytes=64)
-            nc.sync.dma_start(out=t[:].bitcast(I32), in_=words[e].bitcast(I32).rearrange("s p c -> p s c"))
+        def load_words(name, words, e0, e1):
+            t = keep.tile([P, (e1 - e0) * PASSES, 2 * H], U8, name=name, align_bytes=64)
+            nc.sync.dma_start(out=t[:].bitcast(I32), in_=words[e0:e1].bitcast(I32).rearrange("e s p c -> p (e s) c"))
             return t
 
-        def shared_words(name, words):
-            t = keep.tile([P, PASSES, 2 * H], U8, name=name, align_bytes=64)
-            nc.sync.dma_start(out=t[:].bitcast(I32), in_=words[E].bitcast(I32).rearrange("s p c -> p s c"))
-            return t
+        def bank(tag, width):
+            return psum.tile([P, width], F32, name="bank_" + tag, tag=tag, bufs=4 if tag == "b" else 1)
 
-        xs = plane("xs", PASSES * T)
-        FIRST = E - 1
-        s1a = plane("s1a", 2 * PASSES * H)
-        s3a = plane("s3a", 2 * PASSES * H)
-        xp = plane("xp", T)
-        s2 = plane("s2", (E + 1) * N)
-        s1b = plane("s1b", FIRST * PASSES * H)
-        s3b = plane("s3b", FIRST * PASSES * H)
+        xs = plane("xs", PASSES * T, nc.gpsimd)
+        s1a = plane("s1a", (E + 1 - FIRST) * PASSES * H, nc.vector)
+        s3a = plane("s3a", (E + 1 - FIRST) * PASSES * H, nc.vector)
+        s2 = plane("s2", (E + 1) * N, nc.vector)
+        s1b = plane("s1b", FIRST * PASSES * H, nc.vector)
+        s3b = plane("s3b", FIRST * PASSES * H, nc.vector)
 
         offs_sb = keep.tile([P, S // 16], U16, name="offs_sb")
         nc.sync.dma_start(offs_sb[:], offs)
         xw = [keep.tile([P, T], U32, name="xw%d" % o, align_bytes=64) for o in range(PASSES)]
-        nc.sync.dma_start(out=xw[0][:].bitcast(I32), in_=x_words[0].rearrange("p t r -> p (t r)").bitcast(I32))
+        rows1a = w1_scales[FIRST:].rearrange("e s q c -> (e s) q c")
         load_scales(nc.sync, xs, x_scales)
-        w1s = shared_words("w1s", w1_words)
+        load_scales(nc.sync, s1a, rows1a, range(1))
+        nc.sync.dma_start(out=xw[0][:].bitcast(I32), in_=x_words[0].rearrange("p t r -> p (t r)").bitcast(I32))
+        w1s = load_words("w1s", w1_words, E, E + 1)
+        load_scales(nc.sync, s1a, rows1a, range(1, 4))
         nc.sync.dma_start(out=xw[1][:].bitcast(I32), in_=x_words[1].rearrange("p t r -> p (t r)").bitcast(I32))
-        load_scales(nc.sync, s1a, w1_scales[FIRST:].rearrange("e s q c -> (e s) q c"))
-        w3s = shared_words("w3s", w3_words)
+        w3s = load_words("w3s", w3_words, E, E + 1)
         load_scales(nc.sync, s3a, w3_scales[FIRST:].rearrange("e s q c -> (e s) q c"))
+        pairs = {}
+        pairs[2] = (load_words("w1c", w1_words, 4, 6), load_words("w3c", w3_words, 4, 6))
+        load_scales(nc.sync, s1b, w1_scales[:FIRST].rearrange("e s q c -> (e s) q c"))
+        load_scales(nc.sync, s3b, w3_scales[:FIRST].rearrange("e s q c -> (e s) q c"))
+        w2 = keep.tile([P, E + 1, 2 * N], U8, name="w2", align_bytes=64)
+        nc.sync.dma_start(out=w2[:].bitcast(I32), in_=w2_words.bitcast(I32).rearrange("e s p c -> p (e s) c"))
+        load_scales(nc.gpsimd, s2, w2_scales.rearrange("e s q c -> (e s) q c"))
+        pairs[1] = (load_words("w1b", w1_words, 2, 4), load_words("w3b", w3_words, 2, 4))
+        pairs[0] = (load_words("w1a", w1_words, 0, 2), load_words("w3a", w3_words, 0, 2))
+        pos_sb = []
+        for name, pos in (("pos1_sb", pos1), ("pos2_sb", pos2)):
+            t = keep.tile([P, T // 16], U16, name=name)
+            nc.sync.dma_start(t[:], pos)
+            pos_sb.append(t)
+        gate_sb = keep.tile([P, 2, T], F32, name="gate_sb")
+        nc.sync.dma_start(out=gate_sb[:], in_=gate.rearrange("j p t -> p j t"))
         ident = keep.tile([P, P], F32, name="ident")
         make_identity(nc, ident[:])
 
         y = keep.tile([P, S], F32, name="y")
-        w2 = keep.tile([P, E + 1, 2 * N], U8, name="w2", align_bytes=64)
-        ys0 = keep.tile([P, C], F32, name="ys0")
+        gathered = {}
 
-        def gather_bytes_apart(first):
-            tiles = []
+        def gather(sort, e, tag):
+            t = work.tile([P, PASSES, C], U32 if sort == "W" else U8, name="g%s%d" % (sort, e), tag=tag, align_bytes=64)
             for o in range(PASSES):
-                g = keep.tile([P, 2 * C], U8, name="ga%d" % o, align_bytes=64)
-                nc.vector.tensor_copy(g[:], xs[:, o * T : (o + 1) * T].indirect(offs_sb[:, first * 16 : (first + 2) * 16]))
-                tiles.append(g)
-            return tiles
+                window = xw[o][:] if sort == "W" else xs[:, o * T : (o + 1) * T]
+                nc.vector.tensor_copy(t[:, o, :], window.indirect(offs_sb[:, e * 16 : (e + 1) * 16]))
+            gathered[(sort, e)] = t
 
-        def gather_bytes(first):
-            g = ring.tile([P, 2 * C], U8, name="gb", tag="gb", bufs=2, align_bytes=64)
-            nc.vector.tensor_copy(g[:], xp[:].indirect(offs_sb[:, first * 16 : (first + 2) * 16]))
-            m = ring.tile([P, 2 * C], U8, name="mb", tag="mb", bufs=2, align_bytes=64)
-            nc.gpsimd.dma_start(out=m[0:64, :].bitcast(I32), in_=g[4:68, :].bitcast(I32))
-            nc.gpsimd.dma_start(out=m[64:128, :].bitcast(I32), in_=g[8:72, :].bitcast(I32))
-            return g, m
+        for e in reversed(range(E)):
+            for sort in ("W", "B"):
+                if (sort, e) not in GATES:
+                    gather(sort, e, "free%s%d" % (sort, e))
 
-        def gather_words(e):
-            tiles = []
-            for o in range(PASSES):
-                g = ring.tile([P, C], U32, name="gw%d" % o, tag="gw%d" % o, bufs=2, align_bytes=64)
-                nc.vector.tensor_copy(g[:], xw[o][:].indirect(offs_sb[:, e * 16 : (e + 1) * 16]))
-                tiles.append(g)
-            return tiles
+        hidden = {}
+        quantised = {}
+        shared_sums = {}
+        done = []
 
-        def first_layer(words, scales, w1, w3, sc1, sc3):
-            hs = []
-            for j in range(2):
-                cols = slice(j * P, (j + 1) * P)
-                a = psum.tile([P, H], F32, name="a", tag="a", bufs=2)
-                b = psum.tile([P, H], F32, name="b", tag="b", bufs=3)
-                for acc, w, sc in ((a, w1, sc1), (b, w3, sc3)):
-                    for o in range(PASSES):
-                        nc.tensor.matmul_mx(
-                            out=acc[:],
-                            lhsT=words[o][:, cols].bitcast(FP8X4),
-                            lhsT_scale=scales[o][:, cols],
-                            rhs=w[:, o, :].bitcast(FP4X4),
-                            rhs_scale=sc[:, o * H : (o + 1) * H],
-                            start=(o == 0),
-                            stop=(o == PASSES - 1),
-                        )
-                g = ring.tile([P, H], F32, name="g", tag="g", bufs=3)
-                nc.scalar.activation(
-                    out=g[:].rearrange("q (u p e) -> q u p e", u=2, e=2),
-                    in_=a[:].rearrange("q (p u e) -> q u p e", u=2, e=2),
-                    func=GELU,
-                )
-                h = ring.tile([P, H], BF16, name="h", tag="h", bufs=4, align_bytes=64)
-                nc.vector.tensor_tensor(
-                    out=h[:].rearrange("q (u p e) -> q u p e", u=2, e=2),
-                    in0=b[:].rearrange("q (p u e) -> q u p e", u=2, e=2),
-                    in1=g[:].rearrange("q (u p e) -> q u p e", u=2, e=2),
-                    op=MULT,
-                )
-                hs.append(h)
-            return hs
+        def first_layer(n, j):
+            kind, i = UNITS[n]
+            if kind == "s":
+                c0 = i * C + j * P
+                words = [xw[o][:, c0 : c0 + P] for o in range(PASSES)]
+                scales = [xs[:, o * T + c0 : o * T + c0 + P] for o in range(PASSES)]
+                ws = [w1s, w3s]
+                row, e = 0, E
+            else:
+                words = [gathered[("W", i)][:, o, j * P : (j + 1) * P] for o in range(PASSES)]
+                scales = [gathered[("B", i)][:, o, j * P : (j + 1) * P] for o in range(PASSES)]
+                ws = pairs[i // 2]
+                row, e = (i % 2) * PASSES, i
+            planes, col = ((s1a, s3a), (e - FIRST) * PASSES * H) if e >= FIRST else ((s1b, s3b), e * PASSES * H)
+            a = bank("A%d" % ((j - n) % 3), H)
+            b = bank("b", H)
+            for acc, w, sc in zip((a, b), ws, planes):
+                for o in range(PASSES):
+                    nc.tensor.matmul_mx(
+                        out=acc[:],
+                        lhsT=words[o].bitcast(FP8X4),
+                        lhsT_scale=scales[o],
+                        rhs=w[:, row + o, :].bitcast(FP4X4),
+                        rhs_scale=sc[:, col + o * H : col + (o + 1) * H],
+                        start=(o == 0),
+                        stop=(o == PASSES - 1),
+                    )
+            m = len(done)
+            done.append((n, j))
+            g = work.tile([P, H], F32, name="g%d" % m, tag="g%d" % m, align_bytes=64)
+            nc.scalar.activation(
+                out=g[:].rearrange("q (u p e) -> q u p e", u=2, e=2),
+                in_=a[:].rearrange("q (p u e) -> q u p e", u=2, e=2),
+                func=GELU,
+            )
+            h = work.tile([P, H], BF16, name="h%d" % m, align_bytes=64)
+            nc.vector.tensor_tensor(
+                out=h[:].rearrange("q (u p e) -> q u p e", u=2, e=2),
+                in0=b[:].rearrange("q (p u e) -> q u p e", u=2, e=2),
+                in1=g[:].rearrange("q (u p e) -> q u p e", u=2, e=2),
+                op=MULT,
+            )
+            hidden[(n, j)] = h
+            for key, after in GATES.items():
+                if after % 100 == m:
+                    gather(key[0], key[1], "g%d" % m if after < 100 else "h%d" % m)
 
-        def turn_and_quantise(hs):
-            tr = psum.tile([P, 4, P], F32, name="tr", tag="tr", bufs=1)
-            for j in range(2):
+        def turn_and_quantise(n, tag):
+            tr = bank(tag, 4 * P)
+            for j in (1, 0):
                 for u in range(2):
-                    nc.tensor.transpose(tr[:, 2 * j + u, :], hs[j][:].bitcast(F32)[:, u * P : (u + 1) * P], ident[:])
-            ht = ring.tile([P, 4 * C], BF16, name="ht", tag="ht", bufs=2, align_bytes=64)
+                    nc.tensor.transpose(
+                        tr[:, (2 * j + u) * P : (2 * j + u + 1) * P],
+                        hidden[(n, j)][:].bitcast(F32)[:, u * P : (u + 1) * P],
+                        ident[:],
+                    )
+            ht = work.tile([P, 4 * C], BF16, name="ht%d" % n, align_bytes=64)
             nc.scalar.copy(
                 out=ht[:].bitcast(F32).rearrange("p (j s u) -> p j s u", j=2, u=2),
-                in_=tr[:].rearrange("p (j u) s -> p j s u", u=2),
+                in_=tr[:].rearrange("p (j u s) -> p j s u", j=2, u=2),
             )
-            hq = ring.tile([P, C], U32, name="hq", tag="hq", bufs=2, align_bytes=64)
-            hz = ring.tile([P, C], U8, name="hz", tag="hz", bufs=2, align_bytes=64)
+            hq = work.tile([P, C], U32, name="hq%d" % n, align_bytes=64)
+            hz = work.tile([P, C], U8, name="hz%d" % n, align_bytes=64)
             nc.vector.quantize_mx(out=hq[:].bitcast(FP8X4), scales=hz[:], in_=ht[:])
-            return hq, hz
+            quantised[n] = (hq, hz)
 
-        def second_layer(e, hq, hz):
-            acc = psum.tile([P, C], F32, name="yacc", tag="yacc", bufs=2)
+        def second_layer(n, tag):
+            kind, i = UNITS[n]
+            e = E if kind == "s" else i
+            hq, hz = quantised[n]
+            acc = bank(tag, C)
             nc.tensor.matmul_mx(
                 out=acc[:],
                 lhsT=w2[:, e, :].bitcast(FP4X4),
@@ -161,105 +193,35 @@ def tile_moe_shr_glu_gelu_kernel(
                 start=True,
                 stop=True,
             )
-            return acc
-
-        units = [("s", 0)] + [("e", e) for e in reversed(range(E))] + [("s", 1), ("s", 2)]
-        routed = [i for kind, i in units if kind == "e"]
-        weights = {}
-        tokens = {}
-        planes = {}
-
-        def prepare(e):
-            weights[e] = (load_words("w1", w1_words, e), load_words("w3", w3_words, e))
-            tokens[e] = gather_words(e)
-            if e == E - 1:
-                planes[e // 2] = gather_bytes_apart(e - 1)
-            elif e % 2 == 0 and e > 0:
-                planes[e // 2 - 1] = gather_bytes(e - 2)
-
-        prepare(routed[0])
-        load_scales(nc.sync, xp, x_scales[0:1])
-        SECOND = (4, 36, 8, 40)
-        for q in range(4):
-            nc.gpsimd.dma_start(
-                out=xp[SECOND[q] : SECOND[q] + 4, :].bitcast(I32), in_=x_scales[1, 4 * q : 4 * q + 4, :].bitcast(I32)
-            )
-        nc.sync.dma_start(out=w2[:].bitcast(I32), in_=w2_words.bitcast(I32).rearrange("e s p c -> p (e s) c"))
-        load_scales(nc.sync, s2, w2_scales.rearrange("e s q c -> (e s) q c"))
-        load_scales(nc.sync, s1b, w1_scales[:FIRST].rearrange("e s q c -> (e s) q c"))
-        load_scales(nc.sync, s3b, w3_scales[:FIRST].rearrange("e s q c -> (e s) q c"))
-        prepare(routed[1])
-        pos_sb = []
-        for name, pos in (("pos1_sb", pos1), ("pos2_sb", pos2)):
-            t = keep.tile([P, T // 16], U16, name=name)
-            nc.sync.dma_start(t[:], pos)
-            pos_sb.append(t)
-        gate_sb = keep.tile([P, 2, T], F32, name="gate_sb")
-
-        shared_sums = {}
-        hidden = {}
-        quantised = {}
-
-        def stage1(n):
-            kind, i = units[n]
-            if kind == "s":
-                cols = slice(i * C, (i + 1) * C)
-                words = [xw[o][:, cols] for o in range(PASSES)]
-                scales = [xs[:, o * T + i * C : o * T + (i + 1) * C] for o in range(PASSES)]
-                hidden[n] = first_layer(words, scales, w1s, w3s, s1a[:, PASSES * H :], s3a[:, PASSES * H :])
-            else:
-                cols = slice((i % 2) * C, (i % 2 + 1) * C)
-                scales = [t[:, cols] for t in planes[i // 2]]
-                if i >= FIRST:
-                    sc = [t[:, : PASSES * H] for t in (s1a, s3a)]
-                else:
-                    sc = [t[:, i * PASSES * H : (i + 1) * PASSES * H] for t in (s1b, s3b)]
-                hidden[n] = first_layer(tokens[i], scales, weights[i][0], weights[i][1], sc[0], sc[1])
-                nxt = routed.index(i) + 2
-                if nxt < E:
-                    prepare(routed[nxt])
-                if nxt == E:
-                    nc.sync.dma_start(out=gate_sb[:], in_=gate.rearrange("j p t -> p j t"))
-
-        def stage3(n):
-            kind, i = units[n]
-            acc = second_layer(E if kind == "s" else i, *quantised[n])
             if kind == "e":
                 nc.scalar.copy(out=y[:, i * C : (i + 1) * C], in_=acc[:])
-            elif i == 0:
-                nc.scalar.copy(out=ys0[:], in_=acc[:])
-                shared_sums[i] = ys0
+            elif i in COPIED:
+                ys = work.tile([P, C], F32, name="ys%d" % i)
+                nc.scalar.copy(out=ys[:], in_=acc[:])
+                shared_sums[i] = ys
             else:
                 shared_sums[i] = acc
 
-        last_routed = units.index(("e", routed[-1]))
-        steps = []
-        for n in range(len(units) + 2):
-            steps.extend([(1, n), (3, n - 2), (2, n - 1)])
-            if n == last_routed:
-                steps.extend([(3, n - 1), (2, n), (3, n)])
-        taken = set()
-        for stage, n in steps:
-            if 0 <= n < len(units) and (stage, n) not in taken:
-                taken.add((stage, n))
-                if stage == 1:
-                    stage1(n)
-                elif stage == 2:
-                    quantised[n] = turn_and_quantise(hidden[n])
-                else:
-                    stage3(n)
+        for step in PLAN:
+            if step[0] == 1:
+                for j in step[2:] or (0, 1):
+                    first_layer(step[1], j)
+            elif step[0] == 2:
+                turn_and_quantise(step[1], step[2])
+            else:
+                second_layer(step[1], step[2])
 
         for c in range(T // C):
             cols = slice(c * C, (c + 1) * C)
             parts = []
             for j in range(2):
-                t = ring.tile([P, C], F32, name="part%d" % j, tag="part%d" % j, bufs=3)
+                t = work.tile([P, C], F32, name="part%d_%d" % (j, c))
                 nc.vector.tensor_tensor(
                     out=t[:], in0=y[:].indirect(pos_sb[j][:, c * 16 : (c + 1) * 16]), in1=gate_sb[:, j, cols], op=MULT
                 )
                 parts.append(t)
-            s = ring.tile([P, C], F32, name="s", tag="s", bufs=3)
+            s = work.tile([P, C], F32, name="s%d" % c)
             nc.vector.tensor_tensor(out=s[:], in0=parts[0][:], in1=parts[1][:], op=ADD)
-            r = ring.tile([P, C], F32, name="r", tag="r", bufs=3)
+            r = work.tile([P, C], F32, name="r%d" % c)
             nc.vector.tensor_tensor(out=r[:], in0=shared_sums[c][:], in1=s[:], op=ADD)
             nc.sync.dma_start(out=out[:, cols], in_=r[:])

@@ -20,11 +20,17 @@ FP4X4 = mybir.dt.float4_e2m1fn_x4
 GELU = mybir.ActivationFunctionType.Gelu_apprx_tanh
 MULT = mybir.AluOpType.mult
 ADD = mybir.AluOpType.add
-FIRST = E - 1
-GATES = {("W", 2): 0, ("B", 2): 2, ("W", 1): 3, ("B", 1): 4, ("W", 0): 6, ("B", 0): 7}
-PLAN = [[1,0],[1,1],[1,2],[2,0,"A1"],[1,3],[2,1,"A0"],[1,4],[2,2,"A2"],[3,0,"A0"],[1,5],[2,3,"A1"],[3,1,"A2"],[1,6,0],[2,4,"y"],[3,2,"A0"],[1,6,1],[2,5,"y"],[3,3,"A1"],[1,7,0],[2,6,"y"],[3,4,"A2"],[3,5,"A1"],[1,7,1],[3,6,"y"],[1,8,0],[2,7,"A0"],[1,8,1],[2,8,"A1"],[3,7,"b"],[3,8,"b"]]
-UNITS = [("s", 0)] + [("e", e) for e in reversed(range(E))] + [("s", 1), ("s", 2)]
-COPIED = (0,)
+EARLY = 3
+UNITS = E + T // C
+WINDOW = 1536
+UP = 3
+FT = ["p0", "g7_1", "g8_0", "g8_1", "h8_0", "h8_1"]
+GW = {1: 2, 3: 1, 4: 0}
+GS = 2
+GROUPS = ((2, 6), (0, 2))
+ORDER = [(E, 0)] + [(e, None) for e in reversed(range(E))] + [(E, 1), (E, 2)]
+LOW = E + 1 - EARLY
+MOVED = 112
 
 
 def tile_moe_shr_glu_gelu_kernel(
@@ -41,95 +47,119 @@ def tile_moe_shr_glu_gelu_kernel(
             engine.memset(t[:].bitcast(I32), 0)
             return t
 
-        def load_scales(queue, t, rows, which=range(4)):
+        def load_scales(queue, t, scales, which=range(4)):
+            rows = scales.rearrange("e s q c -> (e s) q c")
             src = rows.bitcast(I32).rearrange("g (q r) c -> r q g c", r=4)
             dst = t[:].bitcast(I32).rearrange("p (g c) -> p g c", g=rows.shape[0])
             for r in which:
                 queue.dma_start(out=dst[r:P:32], in_=src[r])
 
+        weights = {}
+
         def load_words(name, words, e0, e1):
-            t = keep.tile([P, (e1 - e0) * PASSES, 2 * H], U8, name=name, align_bytes=64)
+            t = keep.tile([P, (e1 - e0) * PASSES, 2 * H], U8, name="%s_%d" % (name, e0), align_bytes=64)
             nc.sync.dma_start(out=t[:].bitcast(I32), in_=words[e0:e1].bitcast(I32).rearrange("e s p c -> p (e s) c"))
-            return t
+            for e in range(e0, e1):
+                weights[(name, e)] = (t, (e - e0) * PASSES)
+
+        def move_down(dst, src):
+            nc.sync.dma_start(out=dst[0:MOVED, :].bitcast(I32), in_=src[4 : 4 + MOVED, :].bitcast(I32))
 
         def bank(tag, width):
             return psum.tile([P, width], F32, name="bank_" + tag, tag=tag, bufs=4 if tag == "b" else 1)
 
-        xs = plane("xs", PASSES * T, nc.gpsimd)
-        s1a = plane("s1a", (E + 1 - FIRST) * PASSES * H, nc.vector)
-        s3a = plane("s3a", (E + 1 - FIRST) * PASSES * H, nc.vector)
+        xs = plane("xs", WINDOW, nc.gpsimd)
+        s1a = plane("s1a", EARLY * PASSES * H, nc.vector)
+        s3a = plane("s3a", EARLY * PASSES * H, nc.vector)
+        xs1 = plane("xs1", T, nc.vector)
+        moved = [plane("moved%d" % e0, (e1 - e0) * C, nc.vector) for e0, e1 in GROUPS]
         s2 = plane("s2", (E + 1) * N, nc.vector)
-        s1b = plane("s1b", FIRST * PASSES * H, nc.vector)
-        s3b = plane("s3b", FIRST * PASSES * H, nc.vector)
+        s1b = plane("s1b", (E + 1 - EARLY) * PASSES * H, nc.vector)
+        s3b = plane("s3b", (E + 1 - EARLY) * PASSES * H, nc.vector)
 
         offs_sb = keep.tile([P, S // 16], U16, name="offs_sb")
         nc.sync.dma_start(offs_sb[:], offs)
+        for q in range(4):
+            nc.sync.dma_start(
+                out=xs[32 * q : 32 * q + 4 * PASSES, 0:T].bitcast(I32), in_=x_scales[:, 4 * q : 4 * q + 4, :].bitcast(I32)
+            )
         xw = [keep.tile([P, T], U32, name="xw%d" % o, align_bytes=64) for o in range(PASSES)]
-        rows1a = w1_scales[FIRST:].rearrange("e s q c -> (e s) q c")
-        load_scales(nc.sync, xs, x_scales)
-        load_scales(nc.sync, s1a, rows1a, range(1))
         nc.sync.dma_start(out=xw[0][:].bitcast(I32), in_=x_words[0].rearrange("p t r -> p (t r)").bitcast(I32))
-        w1s = load_words("w1s", w1_words, E, E + 1)
-        load_scales(nc.sync, s1a, rows1a, range(1, 4))
+        load_words("w1", w1_words, E, E + 1)
+        load_scales(nc.sync, s1a, w1_scales[LOW:])
         nc.sync.dma_start(out=xw[1][:].bitcast(I32), in_=x_words[1].rearrange("p t r -> p (t r)").bitcast(I32))
-        w3s = load_words("w3s", w3_words, E, E + 1)
-        load_scales(nc.sync, s3a, w3_scales[FIRST:].rearrange("e s q c -> (e s) q c"))
-        pairs = {}
-        pairs[2] = (load_words("w1c", w1_words, 4, 6), load_words("w3c", w3_words, 4, 6))
-        load_scales(nc.sync, s1b, w1_scales[:FIRST].rearrange("e s q c -> (e s) q c"))
-        load_scales(nc.sync, s3b, w3_scales[:FIRST].rearrange("e s q c -> (e s) q c"))
-        w2 = keep.tile([P, E + 1, 2 * N], U8, name="w2", align_bytes=64)
-        nc.sync.dma_start(out=w2[:].bitcast(I32), in_=w2_words.bitcast(I32).rearrange("e s p c -> p (e s) c"))
-        load_scales(nc.gpsimd, s2, w2_scales.rearrange("e s q c -> (e s) q c"))
-        pairs[1] = (load_words("w1b", w1_words, 2, 4), load_words("w3b", w3_words, 2, 4))
-        pairs[0] = (load_words("w1a", w1_words, 0, 2), load_words("w3a", w3_words, 0, 2))
-        pos_sb = []
-        for name, pos in (("pos1_sb", pos1), ("pos2_sb", pos2)):
-            t = keep.tile([P, T // 16], U16, name=name)
-            nc.sync.dma_start(t[:], pos)
-            pos_sb.append(t)
-        gate_sb = keep.tile([P, 2, T], F32, name="gate_sb")
-        nc.sync.dma_start(out=gate_sb[:], in_=gate.rearrange("j p t -> p j t"))
+        move_down(xs1, xs[:, 0:T])
+        load_words("w3", w3_words, E, E + 1)
+        load_scales(nc.sync, s3a, w3_scales[LOW:])
+        load_scales(nc.gpsimd, s2, w2_scales)
         ident = keep.tile([P, P], F32, name="ident")
         make_identity(nc, ident[:])
 
-        y = keep.tile([P, S], F32, name="y")
-        gathered = {}
+        slot_words = {}
+        slot_scales = {}
 
-        def gather(sort, e, tag):
-            t = work.tile([P, PASSES, C], U32 if sort == "W" else U8, name="g%s%d" % (sort, e), tag=tag, align_bytes=64)
+        def gather_words(e, tag):
+            t = work.tile([P, PASSES, C], U32, name="gw%d" % e, tag=tag, align_bytes=64)
             for o in range(PASSES):
-                window = xw[o][:] if sort == "W" else xs[:, o * T : (o + 1) * T]
-                nc.vector.tensor_copy(t[:, o, :], window.indirect(offs_sb[:, e * 16 : (e + 1) * 16]))
-            gathered[(sort, e)] = t
+                nc.vector.tensor_copy(t[:, o, :], xw[o][:].indirect(offs_sb[:, e * 16 : (e + 1) * 16]))
+            slot_words[e] = t
 
-        for e in reversed(range(E)):
-            for sort in ("W", "B"):
-                if (sort, e) not in GATES:
-                    gather(sort, e, "free%s%d" % (sort, e))
+        def gather_scales(g, tag):
+            e0, e1 = GROUPS[g]
+            t = work.tile([P, (e1 - e0) * C], U8, name="gs%d" % g, tag=tag, align_bytes=64)
+            nc.vector.tensor_copy(t[:], xs[:].indirect(offs_sb[:, e0 * 16 : e1 * 16]))
+            slot_scales[g] = t
 
+        gather_scales(0, "gs0")
+        for e in (5, 4, 3)[:UP]:
+            gather_words(e, "gw%d" % e)
+        load_words("w1", w1_words, 5, 6)
+        load_words("w3", w3_words, 5, 6)
+        move_down(moved[0], slot_scales[0])
+        load_words("w1", w1_words, 4, 5)
+        load_words("w3", w3_words, 4, 5)
+        w2 = keep.tile([P, E + 1, 2 * N], U8, name="w2", align_bytes=64)
+        nc.sync.dma_start(out=w2[:].bitcast(I32), in_=w2_words.bitcast(I32).rearrange("e s p c -> p (e s) c"))
+        load_scales(nc.sync, s1b, w1_scales[:LOW])
+        load_scales(nc.sync, s3b, w3_scales[:LOW])
+        load_words("w1", w1_words, 3, 4)
+        load_words("w3", w3_words, 3, 4)
+
+        y = keep.tile([P, S], F32, name="y")
+        pos_sb = [keep.tile([P, T // 16], U16, name="pos%d_sb" % j) for j in range(2)]
+        gate_sb = keep.tile([P, 2, T], F32, name="gate_sb")
         hidden = {}
         quantised = {}
         shared_sums = {}
-        done = []
+
+        def late_loads():
+            load_words("w1", w1_words, 2, 3)
+            load_words("w3", w3_words, 2, 3)
+            load_words("w1", w1_words, 1, 2)
+            load_words("w3", w3_words, 1, 2)
+            move_down(moved[1], slot_scales[1])
+            load_words("w1", w1_words, 0, 1)
+            load_words("w3", w3_words, 0, 1)
+            nc.sync.dma_start(pos_sb[0][:], pos1)
+            nc.sync.dma_start(pos_sb[1][:], pos2)
+            nc.sync.dma_start(out=gate_sb[:], in_=gate.rearrange("j p t -> p j t"))
 
         def first_layer(n, j):
-            kind, i = UNITS[n]
-            if kind == "s":
-                c0 = i * C + j * P
+            e, c = ORDER[n]
+            if e == E:
+                c0 = c * C + j * P
                 words = [xw[o][:, c0 : c0 + P] for o in range(PASSES)]
-                scales = [xs[:, o * T + c0 : o * T + c0 + P] for o in range(PASSES)]
-                ws = [w1s, w3s]
-                row, e = 0, E
+                scales = [t[:, c0 : c0 + P] for t in (xs, xs1)]
             else:
-                words = [gathered[("W", i)][:, o, j * P : (j + 1) * P] for o in range(PASSES)]
-                scales = [gathered[("B", i)][:, o, j * P : (j + 1) * P] for o in range(PASSES)]
-                ws = pairs[i // 2]
-                row, e = (i % 2) * PASSES, i
-            planes, col = ((s1a, s3a), (e - FIRST) * PASSES * H) if e >= FIRST else ((s1b, s3b), e * PASSES * H)
+                grp = 0 if e >= GROUPS[0][0] else 1
+                c0 = (e - GROUPS[grp][0]) * C + j * P
+                words = [slot_words[e][:, o, j * P : (j + 1) * P] for o in range(PASSES)]
+                scales = [t[:, c0 : c0 + P] for t in (slot_scales[grp], moved[grp])]
+            planes, col = ((s1a, s3a), (e - LOW) * PASSES * H) if e >= LOW else ((s1b, s3b), e * PASSES * H)
             a = bank("A%d" % ((j - n) % 3), H)
             b = bank("b", H)
-            for acc, w, sc in zip((a, b), ws, planes):
+            for acc, name, sc in zip((a, b), ("w1", "w3"), planes):
+                w, row = weights[(name, e)]
                 for o in range(PASSES):
                     nc.tensor.matmul_mx(
                         out=acc[:],
@@ -140,15 +170,13 @@ def tile_moe_shr_glu_gelu_kernel(
                         start=(o == 0),
                         stop=(o == PASSES - 1),
                     )
-            m = len(done)
-            done.append((n, j))
-            g = work.tile([P, H], F32, name="g%d" % m, tag="g%d" % m, align_bytes=64)
+            g = work.tile([P, H], F32, name="g%d_%d" % (n, j), tag="g%d_%d" % (n, j), align_bytes=64)
             nc.scalar.activation(
                 out=g[:].rearrange("q (u p e) -> q u p e", u=2, e=2),
                 in_=a[:].rearrange("q (p u e) -> q u p e", u=2, e=2),
                 func=GELU,
             )
-            h = work.tile([P, H], BF16, name="h%d" % m, align_bytes=64)
+            h = work.tile([P, H], BF16, name="h%d_%d" % (n, j), tag="h%d_%d" % (n, j), align_bytes=64)
             nc.vector.tensor_tensor(
                 out=h[:].rearrange("q (u p e) -> q u p e", u=2, e=2),
                 in0=b[:].rearrange("q (p u e) -> q u p e", u=2, e=2),
@@ -156,34 +184,33 @@ def tile_moe_shr_glu_gelu_kernel(
                 op=MULT,
             )
             hidden[(n, j)] = h
-            for key, after in GATES.items():
-                if after % 100 == m:
-                    gather(key[0], key[1], "g%d" % m if after < 100 else "h%d" % m)
 
-        def turn_and_quantise(n, tag):
-            tr = bank(tag, 4 * P)
-            for j in (1, 0):
+        def turn_and_quantise(n, halves, tag):
+            width = len(halves) * P
+            name = "%d_%d" % (n, halves[0])
+            tr = bank(tag, 2 * width)
+            for i in reversed(range(len(halves))):
                 for u in range(2):
                     nc.tensor.transpose(
-                        tr[:, (2 * j + u) * P : (2 * j + u + 1) * P],
-                        hidden[(n, j)][:].bitcast(F32)[:, u * P : (u + 1) * P],
+                        tr[:, (2 * i + u) * P : (2 * i + u + 1) * P],
+                        hidden[(n, halves[i])][:].bitcast(F32)[:, u * P : (u + 1) * P],
                         ident[:],
                     )
-            ht = work.tile([P, 4 * C], BF16, name="ht%d" % n, align_bytes=64)
+            ht = work.tile([P, 4 * width], BF16, name="ht" + name, align_bytes=64)
             nc.scalar.copy(
-                out=ht[:].bitcast(F32).rearrange("p (j s u) -> p j s u", j=2, u=2),
-                in_=tr[:].rearrange("p (j u s) -> p j s u", j=2, u=2),
+                out=ht[:].bitcast(F32).rearrange("p (j s u) -> p j s u", s=P, u=2),
+                in_=tr[:].rearrange("p (j u s) -> p j s u", s=P, u=2),
             )
-            hq = work.tile([P, C], U32, name="hq%d" % n, align_bytes=64)
-            hz = work.tile([P, C], U8, name="hz%d" % n, align_bytes=64)
+            hq = work.tile([P, width], U32, name="hq" + name, align_bytes=64)
+            hz = work.tile([P, width], U8, name="hz" + name, align_bytes=64)
             nc.vector.quantize_mx(out=hq[:].bitcast(FP8X4), scales=hz[:], in_=ht[:])
-            quantised[n] = (hq, hz)
+            quantised[(n, halves)] = (hq, hz)
 
-        def second_layer(n, tag):
-            kind, i = UNITS[n]
-            e = E if kind == "s" else i
-            hq, hz = quantised[n]
-            acc = bank(tag, C)
+        def second_layer(n, halves, tag):
+            e, c = ORDER[n]
+            width = len(halves) * P
+            hq, hz = quantised[(n, halves)]
+            acc = bank(tag, width)
             nc.tensor.matmul_mx(
                 out=acc[:],
                 lhsT=w2[:, e, :].bitcast(FP4X4),
@@ -193,35 +220,63 @@ def tile_moe_shr_glu_gelu_kernel(
                 start=True,
                 stop=True,
             )
-            if kind == "e":
-                nc.scalar.copy(out=y[:, i * C : (i + 1) * C], in_=acc[:])
-            elif i in COPIED:
-                ys = work.tile([P, C], F32, name="ys%d" % i)
+            if e < E:
+                c0 = e * C + halves[0] * P
+                nc.scalar.copy(out=y[:, c0 : c0 + width], in_=acc[:])
+            elif c == 0:
+                ys = work.tile([P, C], F32, name="ys0")
                 nc.scalar.copy(out=ys[:], in_=acc[:])
-                shared_sums[i] = ys
+                shared_sums[c] = ys
             else:
-                shared_sums[i] = acc
+                shared_sums[c] = acc
 
-        for step in PLAN:
-            if step[0] == 1:
-                for j in step[2:] or (0, 1):
-                    first_layer(step[1], j)
-            elif step[0] == 2:
-                turn_and_quantise(step[1], step[2])
-            else:
-                second_layer(step[1], step[2])
+        routed_sums = {}
 
-        for c in range(T // C):
+        def combine(c):
             cols = slice(c * C, (c + 1) * C)
             parts = []
             for j in range(2):
-                t = work.tile([P, C], F32, name="part%d_%d" % (j, c))
+                t = work.tile([P, C], F32, name="part%d_%d" % (j, c), tag=FT[2 * c + j], align_bytes=64)
                 nc.vector.tensor_tensor(
                     out=t[:], in0=y[:].indirect(pos_sb[j][:, c * 16 : (c + 1) * 16]), in1=gate_sb[:, j, cols], op=MULT
                 )
                 parts.append(t)
             s = work.tile([P, C], F32, name="s%d" % c)
             nc.vector.tensor_tensor(out=s[:], in0=parts[0][:], in1=parts[1][:], op=ADD)
+            routed_sums[c] = s
+
+        def finish(c):
             r = work.tile([P, C], F32, name="r%d" % c)
-            nc.vector.tensor_tensor(out=r[:], in0=shared_sums[c][:], in1=s[:], op=ADD)
-            nc.sync.dma_start(out=out[:, cols], in_=r[:])
+            nc.vector.tensor_tensor(out=r[:], in0=shared_sums[c][:], in1=routed_sums[c][:], op=ADD)
+            nc.sync.dma_start(out=out[:, c * C : (c + 1) * C], in_=r[:])
+
+        LAST = E
+        BOTH = (0, 1)
+        for n in range(LAST + 1):
+            first_layer(n, 0)
+            first_layer(n, 1)
+            if n == GS:
+                gather_scales(1, "g%d_1" % n)
+                late_loads()
+            if n in GW:
+                gather_words(GW[n], "g%d_1" % n)
+            if n >= 1:
+                turn_and_quantise(n - 1, BOTH, "A%d" % (-n % 3))
+            if n >= 2:
+                second_layer(n - 2, BOTH, "A%d" % ((1 - n) % 3))
+        turn_and_quantise(LAST, (0,), "y")
+        turn_and_quantise(LAST, (1,), "b")
+        second_layer(LAST - 1, BOTH, "b")
+        second_layer(LAST, (0,), "b")
+        second_layer(LAST, (1,), "y")
+        for n in range(LAST + 1, UNITS):
+            first_layer(n, 0)
+            first_layer(n, 1)
+            if n > LAST + 1:
+                turn_and_quantise(n - 1, BOTH, "A%d" % (-n % 3))
+        turn_and_quantise(UNITS - 1, BOTH, "y")
+        for n in range(LAST + 1, UNITS):
+            second_layer(n, BOTH, "b")
+        for c in range(T // C):
+            combine(c)
+            finish(c)

@@ -5,7 +5,7 @@ from concourse.masks import make_identity
 
 K, T, E, C, H, N = 1024, 768, 6, 256, 512, 128
 P = 128
-PASSES = 2
+PASSES = K // 512
 S = E * C
 FLOPS = 2 * (S + T) * (2 * K * H + H * N)
 
@@ -18,19 +18,22 @@ U8 = mybir.dt.uint8
 FP8X4 = mybir.dt.float8_e4m3fn_x4
 FP4X4 = mybir.dt.float4_e2m1fn_x4
 GELU = mybir.ActivationFunctionType.Gelu_apprx_tanh
+COPY = mybir.ActivationFunctionType.Copy
 MULT = mybir.AluOpType.mult
 ADD = mybir.AluOpType.add
-EARLY = 3
-UNITS = E + T // C
-WINDOW = 1536
-UP = 3
-FT = ["p0", "g7_1", "g8_0", "g8_1", "h8_0", "h8_1"]
-GW = {1: 2, 3: 1, 4: 0}
-GS = 2
-GROUPS = ((2, 6), (0, 2))
-ORDER = [(E, 0)] + [(e, None) for e in reversed(range(E))] + [(E, 1), (E, 2)]
-LOW = E + 1 - EARLY
-MOVED = 112
+
+SHARED = E
+CHUNKS = T // C
+LIST_COLS = C // 16
+UNITS = [(SHARED, 0)] + [(e, None) for e in reversed(range(E))] + [(SHARED, c) for c in range(1, CHUNKS)]
+LAST_ROUTED = E
+LAST = len(UNITS) - 1
+BOTH = (0, 1)
+SPLIT = 4
+SCALE_GROUPS = ((2, 6), (0, 2))
+WINDOW = 2 * T
+MOVED_ROWS = 112
+SUM_BANKS = 4
 
 
 def tile_moe_shr_glu_gelu_kernel(
@@ -47,35 +50,47 @@ def tile_moe_shr_glu_gelu_kernel(
             engine.memset(t[:].bitcast(I32), 0)
             return t
 
-        def load_scales(queue, t, scales, which=range(4)):
-            rows = scales.rearrange("e s q c -> (e s) q c")
+        def load_planes(queue, t, scales):
+            rows = scales.rearrange("e s f c -> (e s) f c")
             src = rows.bitcast(I32).rearrange("g (q r) c -> r q g c", r=4)
             dst = t[:].bitcast(I32).rearrange("p (g c) -> p g c", g=rows.shape[0])
-            for r in which:
+            for r in range(4):
                 queue.dma_start(out=dst[r:P:32], in_=src[r])
 
-        weights = {}
+        w1, w3 = {}, {}
 
-        def load_words(name, words, e0, e1):
-            t = keep.tile([P, (e1 - e0) * PASSES, 2 * H], U8, name="%s_%d" % (name, e0), align_bytes=64)
-            nc.sync.dma_start(out=t[:].bitcast(I32), in_=words[e0:e1].bitcast(I32).rearrange("e s p c -> p (e s) c"))
-            for e in range(e0, e1):
-                weights[(name, e)] = (t, (e - e0) * PASSES)
+        def load_words(tiles, name, words, e):
+            t = keep.tile([P, PASSES, 2 * H], U8, name="%s_%d" % (name, e), align_bytes=64)
+            nc.sync.dma_start(out=t[:].bitcast(I32), in_=words[e : e + 1].bitcast(I32).rearrange("e s p c -> p (e s) c"))
+            tiles[e] = t
+
+        def load_expert(e):
+            load_words(w1, "w1", w1_words, e)
+            load_words(w3, "w3", w3_words, e)
 
         def move_down(dst, src):
-            nc.sync.dma_start(out=dst[0:MOVED, :].bitcast(I32), in_=src[4 : 4 + MOVED, :].bitcast(I32))
+            nc.sync.dma_start(out=dst[0:MOVED_ROWS, :].bitcast(I32), in_=src[4 : 4 + MOVED_ROWS, :].bitcast(I32))
 
         def bank(tag, width):
-            return psum.tile([P, width], F32, name="bank_" + tag, tag=tag, bufs=4 if tag == "b" else 1)
+            return psum.tile([P, width], F32, name="bank_" + tag, tag=tag, bufs=SUM_BANKS if tag == "sums" else 1)
+
+        def gelu_bank(n, j):
+            return "turn%d" % ((j - n) % 3)
+
+        def gelu_tag(n, j):
+            return "g%d_%d" % (n, j)
+
+        def hidden_tag(n, j):
+            return "h%d_%d" % (n, j)
 
         xs = plane("xs", WINDOW, nc.gpsimd)
-        s1a = plane("s1a", EARLY * PASSES * H, nc.vector)
-        s3a = plane("s3a", EARLY * PASSES * H, nc.vector)
-        xs1 = plane("xs1", T, nc.vector)
-        moved = [plane("moved%d" % e0, (e1 - e0) * C, nc.vector) for e0, e1 in GROUPS]
+        s1_first = plane("s1_first", (E + 1 - SPLIT) * PASSES * H, nc.vector)
+        s3_first = plane("s3_first", (E + 1 - SPLIT) * PASSES * H, nc.vector)
+        xs_second = plane("xs_second", T, nc.vector)
+        slot_second = [plane("slot_second%d" % e0, (e1 - e0) * C, nc.vector) for e0, e1 in SCALE_GROUPS]
         s2 = plane("s2", (E + 1) * N, nc.vector)
-        s1b = plane("s1b", (E + 1 - EARLY) * PASSES * H, nc.vector)
-        s3b = plane("s3b", (E + 1 - EARLY) * PASSES * H, nc.vector)
+        s1_rest = plane("s1_rest", SPLIT * PASSES * H, nc.vector)
+        s3_rest = plane("s3_rest", SPLIT * PASSES * H, nc.vector)
 
         offs_sb = keep.tile([P, S // 16], U16, name="offs_sb")
         nc.sync.dma_start(offs_sb[:], offs)
@@ -85,13 +100,13 @@ def tile_moe_shr_glu_gelu_kernel(
             )
         xw = [keep.tile([P, T], U32, name="xw%d" % o, align_bytes=64) for o in range(PASSES)]
         nc.sync.dma_start(out=xw[0][:].bitcast(I32), in_=x_words[0].rearrange("p t r -> p (t r)").bitcast(I32))
-        load_words("w1", w1_words, E, E + 1)
-        load_scales(nc.sync, s1a, w1_scales[LOW:])
+        load_words(w1, "w1", w1_words, SHARED)
+        load_planes(nc.sync, s1_first, w1_scales[SPLIT:])
         nc.sync.dma_start(out=xw[1][:].bitcast(I32), in_=x_words[1].rearrange("p t r -> p (t r)").bitcast(I32))
-        move_down(xs1, xs[:, 0:T])
-        load_words("w3", w3_words, E, E + 1)
-        load_scales(nc.sync, s3a, w3_scales[LOW:])
-        load_scales(nc.gpsimd, s2, w2_scales)
+        move_down(xs_second, xs[:, 0:T])
+        load_words(w3, "w3", w3_words, SHARED)
+        load_planes(nc.sync, s3_first, w3_scales[SPLIT:])
+        load_planes(nc.gpsimd, s2, w2_scales)
         ident = keep.tile([P, P], F32, name="ident")
         make_identity(nc, ident[:])
 
@@ -101,86 +116,90 @@ def tile_moe_shr_glu_gelu_kernel(
         def gather_words(e, tag):
             t = work.tile([P, PASSES, C], U32, name="gw%d" % e, tag=tag, align_bytes=64)
             for o in range(PASSES):
-                nc.vector.tensor_copy(t[:, o, :], xw[o][:].indirect(offs_sb[:, e * 16 : (e + 1) * 16]))
+                nc.vector.tensor_copy(t[:, o, :], xw[o][:].indirect(offs_sb[:, e * LIST_COLS : (e + 1) * LIST_COLS]))
             slot_words[e] = t
 
-        def gather_scales(g, tag):
-            e0, e1 = GROUPS[g]
-            t = work.tile([P, (e1 - e0) * C], U8, name="gs%d" % g, tag=tag, align_bytes=64)
-            nc.vector.tensor_copy(t[:], xs[:].indirect(offs_sb[:, e0 * 16 : e1 * 16]))
-            slot_scales[g] = t
+        def gather_scales(grp, tag):
+            e0, e1 = SCALE_GROUPS[grp]
+            t = work.tile([P, (e1 - e0) * C], U8, name="gs%d" % grp, tag=tag, align_bytes=64)
+            nc.vector.tensor_copy(t[:], xs[:].indirect(offs_sb[:, e0 * LIST_COLS : e1 * LIST_COLS]))
+            slot_scales[grp] = t
 
         gather_scales(0, "gs0")
-        for e in (5, 4, 3)[:UP]:
+        for e, chunk in UNITS[1:3]:
             gather_words(e, "gw%d" % e)
-        load_words("w1", w1_words, 5, 6)
-        load_words("w3", w3_words, 5, 6)
-        move_down(moved[0], slot_scales[0])
-        load_words("w1", w1_words, 4, 5)
-        load_words("w3", w3_words, 4, 5)
+        load_expert(UNITS[1][0])
+        move_down(slot_second[0], slot_scales[0])
+        load_expert(UNITS[2][0])
         w2 = keep.tile([P, E + 1, 2 * N], U8, name="w2", align_bytes=64)
         nc.sync.dma_start(out=w2[:].bitcast(I32), in_=w2_words.bitcast(I32).rearrange("e s p c -> p (e s) c"))
-        load_scales(nc.sync, s1b, w1_scales[:LOW])
-        load_scales(nc.sync, s3b, w3_scales[:LOW])
-        load_words("w1", w1_words, 3, 4)
-        load_words("w3", w3_words, 3, 4)
+        load_planes(nc.sync, s1_rest, w1_scales[:SPLIT])
+        load_planes(nc.sync, s3_rest, w3_scales[:SPLIT])
+
+        gate_rows = keep.tile([P, P], F32, name="gate_rows")
+        nc.gpsimd.memset(gate_rows[:], 0.0)
+        gate_cols = keep.tile([P, 4], F32, name="gate_cols")
+        nc.sync.dma_start(out=gate_rows[0:4, :], in_=gate[:, 0, 0:C].rearrange("j (i t) -> j i t", t=P))
+        gate_turned = bank("spare", P)
+        nc.tensor.transpose(gate_turned[:], gate_rows[:], ident[:])
+        nc.scalar.copy(out=gate_cols[:], in_=gate_turned[:, 0:4])
+        load_expert(UNITS[3][0])
 
         y = keep.tile([P, S], F32, name="y")
         pos_sb = [keep.tile([P, T // 16], U16, name="pos%d_sb" % j) for j in range(2)]
-        gate_sb = keep.tile([P, 2, T], F32, name="gate_sb")
+        gate_sb = keep.tile([P, 2, T - C], F32, name="gate_sb")
         hidden = {}
         quantised = {}
         shared_sums = {}
 
         def late_loads():
-            load_words("w1", w1_words, 2, 3)
-            load_words("w3", w3_words, 2, 3)
-            load_words("w1", w1_words, 1, 2)
-            load_words("w3", w3_words, 1, 2)
-            move_down(moved[1], slot_scales[1])
-            load_words("w1", w1_words, 0, 1)
-            load_words("w3", w3_words, 0, 1)
+            load_expert(UNITS[4][0])
+            load_expert(UNITS[5][0])
+            move_down(slot_second[1], slot_scales[1])
+            load_expert(UNITS[6][0])
             nc.sync.dma_start(pos_sb[0][:], pos1)
             nc.sync.dma_start(pos_sb[1][:], pos2)
-            nc.sync.dma_start(out=gate_sb[:], in_=gate.rearrange("j p t -> p j t"))
+            nc.sync.dma_start(out=gate_sb[:], in_=gate[:, :, C:].rearrange("j p t -> p j t"))
 
         def first_layer(n, j):
-            e, c = ORDER[n]
-            if e == E:
-                c0 = c * C + j * P
+            e, chunk = UNITS[n]
+            if e == SHARED:
+                c0 = chunk * C + j * P
                 words = [xw[o][:, c0 : c0 + P] for o in range(PASSES)]
-                scales = [t[:, c0 : c0 + P] for t in (xs, xs1)]
+                scales = [t[:, c0 : c0 + P] for t in (xs, xs_second)]
             else:
-                grp = 0 if e >= GROUPS[0][0] else 1
-                c0 = (e - GROUPS[grp][0]) * C + j * P
+                grp = 0 if e >= SCALE_GROUPS[0][0] else 1
+                c0 = (e - SCALE_GROUPS[grp][0]) * C + j * P
                 words = [slot_words[e][:, o, j * P : (j + 1) * P] for o in range(PASSES)]
-                scales = [t[:, c0 : c0 + P] for t in (slot_scales[grp], moved[grp])]
-            planes, col = ((s1a, s3a), (e - LOW) * PASSES * H) if e >= LOW else ((s1b, s3b), e * PASSES * H)
-            a = bank("A%d" % ((j - n) % 3), H)
-            b = bank("b", H)
-            for acc, name, sc in zip((a, b), ("w1", "w3"), planes):
-                w, row = weights[(name, e)]
+                scales = [t[:, c0 : c0 + P] for t in (slot_scales[grp], slot_second[grp])]
+            if e >= SPLIT:
+                planes, col = (s1_first, s3_first), (e - SPLIT) * PASSES * H
+            else:
+                planes, col = (s1_rest, s3_rest), e * PASSES * H
+            a = bank(gelu_bank(n, j), H)
+            b = bank("sums", H)
+            for acc, w, w_plane in zip((a, b), (w1[e], w3[e]), planes):
                 for o in range(PASSES):
                     nc.tensor.matmul_mx(
                         out=acc[:],
                         lhsT=words[o].bitcast(FP8X4),
                         lhsT_scale=scales[o],
-                        rhs=w[:, row + o, :].bitcast(FP4X4),
-                        rhs_scale=sc[:, col + o * H : col + (o + 1) * H],
+                        rhs=w[:, o, :].bitcast(FP4X4),
+                        rhs_scale=w_plane[:, col + o * H : col + (o + 1) * H],
                         start=(o == 0),
                         stop=(o == PASSES - 1),
                     )
-            g = work.tile([P, H], F32, name="g%d_%d" % (n, j), tag="g%d_%d" % (n, j), align_bytes=64)
+            g = work.tile([P, H], F32, name=gelu_tag(n, j), tag=gelu_tag(n, j), align_bytes=64)
             nc.scalar.activation(
-                out=g[:].rearrange("q (u p e) -> q u p e", u=2, e=2),
-                in_=a[:].rearrange("q (p u e) -> q u p e", u=2, e=2),
+                out=g[:].rearrange("q (u p v) -> q u p v", u=2, v=2),
+                in_=a[:].rearrange("q (p u v) -> q u p v", u=2, v=2),
                 func=GELU,
             )
-            h = work.tile([P, H], BF16, name="h%d_%d" % (n, j), tag="h%d_%d" % (n, j), align_bytes=64)
+            h = work.tile([P, H], BF16, name=hidden_tag(n, j), tag=hidden_tag(n, j), align_bytes=64)
             nc.vector.tensor_tensor(
-                out=h[:].rearrange("q (u p e) -> q u p e", u=2, e=2),
-                in0=b[:].rearrange("q (p u e) -> q u p e", u=2, e=2),
-                in1=g[:].rearrange("q (u p e) -> q u p e", u=2, e=2),
+                out=h[:].rearrange("q (u p v) -> q u p v", u=2, v=2),
+                in0=b[:].rearrange("q (p u v) -> q u p v", u=2, v=2),
+                in1=g[:].rearrange("q (u p v) -> q u p v", u=2, v=2),
                 op=MULT,
             )
             hidden[(n, j)] = h
@@ -188,18 +207,18 @@ def tile_moe_shr_glu_gelu_kernel(
         def turn_and_quantise(n, halves, tag):
             width = len(halves) * P
             name = "%d_%d" % (n, halves[0])
-            tr = bank(tag, 2 * width)
+            h_turned = bank(tag, 2 * width)
             for i in reversed(range(len(halves))):
                 for u in range(2):
                     nc.tensor.transpose(
-                        tr[:, (2 * i + u) * P : (2 * i + u + 1) * P],
+                        h_turned[:, (2 * i + u) * P : (2 * i + u + 1) * P],
                         hidden[(n, halves[i])][:].bitcast(F32)[:, u * P : (u + 1) * P],
                         ident[:],
                     )
             ht = work.tile([P, 4 * width], BF16, name="ht" + name, align_bytes=64)
             nc.scalar.copy(
-                out=ht[:].bitcast(F32).rearrange("p (j s u) -> p j s u", s=P, u=2),
-                in_=tr[:].rearrange("p (j u s) -> p j s u", s=P, u=2),
+                out=ht[:].bitcast(F32).rearrange("p (i s u) -> p i s u", s=P, u=2),
+                in_=h_turned[:].rearrange("p (i u s) -> p i s u", s=P, u=2),
             )
             hq = work.tile([P, width], U32, name="hq" + name, align_bytes=64)
             hz = work.tile([P, width], U8, name="hz" + name, align_bytes=64)
@@ -207,76 +226,118 @@ def tile_moe_shr_glu_gelu_kernel(
             quantised[(n, halves)] = (hq, hz)
 
         def second_layer(n, halves, tag):
-            e, c = ORDER[n]
+            e, chunk = UNITS[n]
             width = len(halves) * P
             hq, hz = quantised[(n, halves)]
+            w2_words_e = w2[:, e, :].bitcast(FP4X4)
+            w2_plane = s2[:, e * N : (e + 1) * N]
             acc = bank(tag, width)
+            if chunk == 0:
+                for i in halves:
+                    nc.tensor.matmul_mx(
+                        out=acc[:, i * N : (i + 1) * N],
+                        lhsT=hq[:, i * P : (i + 1) * P].bitcast(FP8X4),
+                        lhsT_scale=hz[:, i * P : (i + 1) * P],
+                        rhs=w2_words_e,
+                        rhs_scale=w2_plane,
+                        start=True,
+                        stop=True,
+                    )
+                ys = work.tile([P, C], F32, name="ys0")
+                nc.scalar.copy(out=ys[:], in_=acc[:])
+                shared_sums[chunk] = ys
+                return
             nc.tensor.matmul_mx(
                 out=acc[:],
-                lhsT=w2[:, e, :].bitcast(FP4X4),
-                lhsT_scale=s2[:, e * N : (e + 1) * N],
+                lhsT=w2_words_e,
+                lhsT_scale=w2_plane,
                 rhs=hq[:].bitcast(FP8X4),
                 rhs_scale=hz[:],
                 start=True,
                 stop=True,
             )
-            if e < E:
+            if e == SHARED:
+                shared_sums[chunk] = acc
+            else:
                 c0 = e * C + halves[0] * P
                 nc.scalar.copy(out=y[:, c0 : c0 + width], in_=acc[:])
-            elif c == 0:
-                ys = work.tile([P, C], F32, name="ys0")
-                nc.scalar.copy(out=ys[:], in_=acc[:])
-                shared_sums[c] = ys
-            else:
-                shared_sums[c] = acc
 
-        routed_sums = {}
+        part_tags = ["part0", gelu_tag(LAST - 1, 1)] + [tag(LAST, j) for tag in (gelu_tag, hidden_tag) for j in BOTH]
 
-        def combine(c):
-            cols = slice(c * C, (c + 1) * C)
+        def part_tile(chunk, j):
+            return work.tile([P, C], F32, name="part%d_%d" % (j, chunk), tag=part_tags[2 * chunk + j], align_bytes=64)
+
+        def routed_results(chunk, j):
+            return y[:].indirect(pos_sb[j][:, chunk * LIST_COLS : (chunk + 1) * LIST_COLS])
+
+        def combine_turned(part_banks, total_bank):
+            terms = [shared_sums[0]]
+            for j in range(2):
+                part = part_tile(0, j)
+                nc.vector.tensor_copy(part[:], routed_results(0, j))
+                part_turned = bank(part_banks[j], C)
+                for i in range(2):
+                    nc.tensor.transpose(part_turned[:, i * P : (i + 1) * P], part[:, i * P : (i + 1) * P], ident[:])
+                scaled = work.tile([P, C], F32, name="scaled%d" % j)
+                for i in range(2):
+                    nc.scalar.activation(
+                        out=scaled[:, i * P : (i + 1) * P],
+                        in_=part_turned[:, i * P : (i + 1) * P],
+                        func=COPY,
+                        scale=gate_cols[:, 2 * j + i : 2 * j + i + 1],
+                    )
+                terms.append(scaled)
+            total = bank(total_bank, C)
+            for i in range(2):
+                block = slice(i * P, (i + 1) * P)
+                for m, term in enumerate(terms):
+                    nc.tensor.matmul(
+                        total[:, block], term[:, block], ident[:], start=(m == 0), stop=(m == len(terms) - 1), is_transpose=True
+                    )
+            result = work.tile([P, C], F32, name="result0")
+            nc.scalar.copy(out=result[:], in_=total[:])
+            nc.sync.dma_start(out=out[:, 0:C], in_=result[:])
+
+        def combine(chunk):
             parts = []
             for j in range(2):
-                t = work.tile([P, C], F32, name="part%d_%d" % (j, c), tag=FT[2 * c + j], align_bytes=64)
+                part = part_tile(chunk, j)
                 nc.vector.tensor_tensor(
-                    out=t[:], in0=y[:].indirect(pos_sb[j][:, c * 16 : (c + 1) * 16]), in1=gate_sb[:, j, cols], op=MULT
+                    out=part[:], in0=routed_results(chunk, j), in1=gate_sb[:, j, (chunk - 1) * C : chunk * C], op=MULT
                 )
-                parts.append(t)
-            s = work.tile([P, C], F32, name="s%d" % c)
-            nc.vector.tensor_tensor(out=s[:], in0=parts[0][:], in1=parts[1][:], op=ADD)
-            routed_sums[c] = s
+                parts.append(part)
+            routed = work.tile([P, C], F32, name="routed%d" % chunk)
+            nc.vector.tensor_tensor(out=routed[:], in0=parts[0][:], in1=parts[1][:], op=ADD)
+            result = work.tile([P, C], F32, name="result%d" % chunk)
+            nc.vector.tensor_tensor(out=result[:], in0=shared_sums[chunk][:], in1=routed[:], op=ADD)
+            nc.sync.dma_start(out=out[:, chunk * C : (chunk + 1) * C], in_=result[:])
 
-        def finish(c):
-            r = work.tile([P, C], F32, name="r%d" % c)
-            nc.vector.tensor_tensor(out=r[:], in0=shared_sums[c][:], in1=routed_sums[c][:], op=ADD)
-            nc.sync.dma_start(out=out[:, c * C : (c + 1) * C], in_=r[:])
-
-        LAST = E
-        BOTH = (0, 1)
-        for n in range(LAST + 1):
+        held = [e for e, chunk in UNITS[3:5]] + [None] + [e for e, chunk in UNITS[5:7]]
+        for n in range(LAST_ROUTED + 1):
             first_layer(n, 0)
             first_layer(n, 1)
-            if n == GS:
-                gather_scales(1, "g%d_1" % n)
-                late_loads()
-            if n in GW:
-                gather_words(GW[n], "g%d_1" % n)
+            if n < len(held):
+                if held[n] is None:
+                    gather_scales(1, gelu_tag(n, 1))
+                    late_loads()
+                else:
+                    gather_words(held[n], gelu_tag(n, 1))
             if n >= 1:
-                turn_and_quantise(n - 1, BOTH, "A%d" % (-n % 3))
+                turn_and_quantise(n - 1, BOTH, gelu_bank(n, 0))
             if n >= 2:
-                second_layer(n - 2, BOTH, "A%d" % ((1 - n) % 3))
-        turn_and_quantise(LAST, (0,), "y")
-        turn_and_quantise(LAST, (1,), "b")
-        second_layer(LAST - 1, BOTH, "b")
-        second_layer(LAST, (0,), "b")
-        second_layer(LAST, (1,), "y")
-        for n in range(LAST + 1, UNITS):
+                second_layer(n - 2, BOTH, gelu_bank(n, 1))
+        turn_and_quantise(LAST_ROUTED, (0,), "spare")
+        turn_and_quantise(LAST_ROUTED, (1,), "sums")
+        second_layer(LAST_ROUTED - 1, BOTH, "sums")
+        second_layer(LAST_ROUTED, (0,), "sums")
+        second_layer(LAST_ROUTED, (1,), "spare")
+        for n in (LAST - 1, LAST):
             first_layer(n, 0)
             first_layer(n, 1)
-            if n > LAST + 1:
-                turn_and_quantise(n - 1, BOTH, "A%d" % (-n % 3))
-        turn_and_quantise(UNITS - 1, BOTH, "y")
-        for n in range(LAST + 1, UNITS):
-            second_layer(n, BOTH, "b")
-        for c in range(T // C):
-            combine(c)
-            finish(c)
+        for j in BOTH:
+            turn_and_quantise(LAST - 1 + j, BOTH, gelu_bank(LAST, j))
+        for n in (LAST - 1, LAST):
+            second_layer(n, BOTH, "sums")
+        combine_turned(("spare", gelu_bank(LAST - 1, 1)), "spare")
+        for chunk in range(1, CHUNKS):
+            combine(chunk)

from contextlib import ExitStack

import concourse.mybir as mybir
from concourse.masks import make_identity

K, T, E, C, H, N = 1024, 768, 6, 256, 512, 128
P = 128
PASSES = K // 512
S = E * C
FLOPS = 2 * (S + T) * (2 * K * H + H * N)

F32 = mybir.dt.float32
BF16 = mybir.dt.bfloat16
I32 = mybir.dt.int32
U32 = mybir.dt.uint32
U16 = mybir.dt.uint16
U8 = mybir.dt.uint8
FP8X4 = mybir.dt.float8_e4m3fn_x4
FP4X4 = mybir.dt.float4_e2m1fn_x4
GELU = mybir.ActivationFunctionType.Gelu_apprx_tanh
COPY = mybir.ActivationFunctionType.Copy
MULT = mybir.AluOpType.mult
ADD = mybir.AluOpType.add

SHARED = E
CHUNKS = T // C
LIST_COLS = C // 16
UNITS = [(SHARED, 0)] + [(e, None) for e in reversed(range(E))] + [(SHARED, c) for c in range(1, CHUNKS)]
LAST_ROUTED = E
LAST = len(UNITS) - 1
BOTH = (0, 1)
SPLIT = 4
SCALE_GROUPS = ((2, 6), (0, 2))
WINDOW = 2 * T
MOVED_ROWS = 112
SUM_BANKS = 4


def tile_moe_shr_glu_gelu_kernel(
    tc, x_words, x_scales, w1_words, w1_scales, w3_words, w3_scales, w2_words, w2_scales, gate, offs, pos1, pos2, out
):
    nc = tc.nc
    with ExitStack() as ctx:
        keep = ctx.enter_context(tc.tile_pool(name="keep", bufs=1))
        work = ctx.enter_context(tc.tile_pool(name="work", bufs=1))
        psum = ctx.enter_context(tc.psum_pool(name="psum", bufs=1))

        def plane(name, width, engine):
            t = keep.tile([P, width], U8, name=name, align_bytes=64)
            engine.memset(t[:].bitcast(I32), 0)
            return t

        def load_planes(queue, t, scales):
            rows = scales.rearrange("e s f c -> (e s) f c")
            src = rows.bitcast(I32).rearrange("g (q r) c -> r q g c", r=4)
            dst = t[:].bitcast(I32).rearrange("p (g c) -> p g c", g=rows.shape[0])
            for r in range(4):
                queue.dma_start(out=dst[r:P:32], in_=src[r])

        w1, w3 = {}, {}

        def load_words(tiles, name, words, e):
            t = keep.tile([P, PASSES, 2 * H], U8, name="%s_%d" % (name, e), align_bytes=64)
            nc.sync.dma_start(out=t[:].bitcast(I32), in_=words[e : e + 1].bitcast(I32).rearrange("e s p c -> p (e s) c"))
            tiles[e] = t

        def load_expert(e):
            load_words(w1, "w1", w1_words, e)
            load_words(w3, "w3", w3_words, e)

        def move_down(dst, src):
            nc.sync.dma_start(out=dst[0:MOVED_ROWS, :].bitcast(I32), in_=src[4 : 4 + MOVED_ROWS, :].bitcast(I32))

        def bank(tag, width):
            return psum.tile([P, width], F32, name="bank_" + tag, tag=tag, bufs=SUM_BANKS if tag == "sums" else 1)

        def gelu_bank(n, j):
            return "turn%d" % ((j - n) % 3)

        def gelu_tag(n, j):
            return "g%d_%d" % (n, j)

        def hidden_tag(n, j):
            return "h%d_%d" % (n, j)

        xs = plane("xs", WINDOW, nc.gpsimd)
        s1_first = plane("s1_first", (E + 1 - SPLIT) * PASSES * H, nc.vector)
        s3_first = plane("s3_first", (E + 1 - SPLIT) * PASSES * H, nc.vector)
        xs_second = plane("xs_second", T, nc.vector)
        slot_second = [plane("slot_second%d" % e0, (e1 - e0) * C, nc.vector) for e0, e1 in SCALE_GROUPS]
        s2 = plane("s2", (E + 1) * N, nc.vector)
        s1_rest = plane("s1_rest", SPLIT * PASSES * H, nc.vector)
        s3_rest = plane("s3_rest", SPLIT * PASSES * H, nc.vector)

        offs_sb = keep.tile([P, S // 16], U16, name="offs_sb")
        nc.sync.dma_start(offs_sb[:], offs)
        for q in range(4):
            nc.sync.dma_start(
                out=xs[32 * q : 32 * q + 4 * PASSES, 0:T].bitcast(I32), in_=x_scales[:, 4 * q : 4 * q + 4, :].bitcast(I32)
            )
        xw = [keep.tile([P, T], U32, name="xw%d" % o, align_bytes=64) for o in range(PASSES)]
        nc.sync.dma_start(out=xw[0][:].bitcast(I32), in_=x_words[0].rearrange("p t r -> p (t r)").bitcast(I32))
        load_words(w1, "w1", w1_words, SHARED)
        load_planes(nc.sync, s1_first, w1_scales[SPLIT:])
        nc.sync.dma_start(out=xw[1][:].bitcast(I32), in_=x_words[1].rearrange("p t r -> p (t r)").bitcast(I32))
        move_down(xs_second, xs[:, 0:T])
        load_words(w3, "w3", w3_words, SHARED)
        load_planes(nc.sync, s3_first, w3_scales[SPLIT:])
        load_planes(nc.gpsimd, s2, w2_scales)
        ident = keep.tile([P, P], F32, name="ident")
        make_identity(nc, ident[:])

        slot_words = {}
        slot_scales = {}

        def gather_words(e, tag):
            t = work.tile([P, PASSES, C], U32, name="gw%d" % e, tag=tag, align_bytes=64)
            for o in range(PASSES):
                nc.vector.tensor_copy(t[:, o, :], xw[o][:].indirect(offs_sb[:, e * LIST_COLS : (e + 1) * LIST_COLS]))
            slot_words[e] = t

        def gather_scales(grp, tag):
            e0, e1 = SCALE_GROUPS[grp]
            t = work.tile([P, (e1 - e0) * C], U8, name="gs%d" % grp, tag=tag, align_bytes=64)
            nc.vector.tensor_copy(t[:], xs[:].indirect(offs_sb[:, e0 * LIST_COLS : e1 * LIST_COLS]))
            slot_scales[grp] = t

        gather_scales(0, "gs0")
        for e, chunk in UNITS[1:3]:
            gather_words(e, "gw%d" % e)
        load_expert(UNITS[1][0])
        move_down(slot_second[0], slot_scales[0])
        load_expert(UNITS[2][0])
        w2 = keep.tile([P, E + 1, 2 * N], U8, name="w2", align_bytes=64)
        nc.sync.dma_start(out=w2[:].bitcast(I32), in_=w2_words.bitcast(I32).rearrange("e s p c -> p (e s) c"))
        load_planes(nc.sync, s1_rest, w1_scales[:SPLIT])
        load_planes(nc.sync, s3_rest, w3_scales[:SPLIT])

        gate_rows = keep.tile([P, P], F32, name="gate_rows")
        nc.gpsimd.memset(gate_rows[:], 0.0)
        gate_cols = keep.tile([P, 4], F32, name="gate_cols")
        nc.sync.dma_start(out=gate_rows[0:4, :], in_=gate[:, 0, 0:C].rearrange("j (i t) -> j i t", t=P))
        gate_turned = bank("spare", P)
        nc.tensor.transpose(gate_turned[:], gate_rows[:], ident[:])
        nc.scalar.copy(out=gate_cols[:], in_=gate_turned[:, 0:4])
        load_expert(UNITS[3][0])

        y = keep.tile([P, S], F32, name="y")
        pos_sb = [keep.tile([P, T // 16], U16, name="pos%d_sb" % j) for j in range(2)]
        gate_sb = keep.tile([P, 2, T - C], F32, name="gate_sb")
        hidden = {}
        quantised = {}
        shared_sums = {}

        def late_loads():
            load_expert(UNITS[4][0])
            load_expert(UNITS[5][0])
            move_down(slot_second[1], slot_scales[1])
            load_expert(UNITS[6][0])
            nc.sync.dma_start(pos_sb[0][:], pos1)
            nc.sync.dma_start(pos_sb[1][:], pos2)
            nc.sync.dma_start(out=gate_sb[:], in_=gate[:, :, C:].rearrange("j p t -> p j t"))

        def first_layer(n, j):
            e, chunk = UNITS[n]
            if e == SHARED:
                c0 = chunk * C + j * P
                words = [xw[o][:, c0 : c0 + P] for o in range(PASSES)]
                scales = [t[:, c0 : c0 + P] for t in (xs, xs_second)]
            else:
                grp = 0 if e >= SCALE_GROUPS[0][0] else 1
                c0 = (e - SCALE_GROUPS[grp][0]) * C + j * P
                words = [slot_words[e][:, o, j * P : (j + 1) * P] for o in range(PASSES)]
                scales = [t[:, c0 : c0 + P] for t in (slot_scales[grp], slot_second[grp])]
            if e >= SPLIT:
                planes, col = (s1_first, s3_first), (e - SPLIT) * PASSES * H
            else:
                planes, col = (s1_rest, s3_rest), e * PASSES * H
            a = bank(gelu_bank(n, j), H)
            b = bank("sums", H)
            for acc, w, w_plane in zip((a, b), (w1[e], w3[e]), planes):
                for o in range(PASSES):
                    nc.tensor.matmul_mx(
                        out=acc[:],
                        lhsT=words[o].bitcast(FP8X4),
                        lhsT_scale=scales[o],
                        rhs=w[:, o, :].bitcast(FP4X4),
                        rhs_scale=w_plane[:, col + o * H : col + (o + 1) * H],
                        start=(o == 0),
                        stop=(o == PASSES - 1),
                    )
            g = work.tile([P, H], F32, name=gelu_tag(n, j), tag=gelu_tag(n, j), align_bytes=64)
            nc.scalar.activation(
                out=g[:].rearrange("q (u p v) -> q u p v", u=2, v=2),
                in_=a[:].rearrange("q (p u v) -> q u p v", u=2, v=2),
                func=GELU,
            )
            h = work.tile([P, H], BF16, name=hidden_tag(n, j), tag=hidden_tag(n, j), align_bytes=64)
            nc.vector.tensor_tensor(
                out=h[:].rearrange("q (u p v) -> q u p v", u=2, v=2),
                in0=b[:].rearrange("q (p u v) -> q u p v", u=2, v=2),
                in1=g[:].rearrange("q (u p v) -> q u p v", u=2, v=2),
                op=MULT,
            )
            hidden[(n, j)] = h

        def turn_and_quantise(n, halves, tag):
            width = len(halves) * P
            name = "%d_%d" % (n, halves[0])
            h_turned = bank(tag, 2 * width)
            for i in reversed(range(len(halves))):
                for u in range(2):
                    nc.tensor.transpose(
                        h_turned[:, (2 * i + u) * P : (2 * i + u + 1) * P],
                        hidden[(n, halves[i])][:].bitcast(F32)[:, u * P : (u + 1) * P],
                        ident[:],
                    )
            ht = work.tile([P, 4 * width], BF16, name="ht" + name, align_bytes=64)
            nc.scalar.copy(
                out=ht[:].bitcast(F32).rearrange("p (i s u) -> p i s u", s=P, u=2),
                in_=h_turned[:].rearrange("p (i u s) -> p i s u", s=P, u=2),
            )
            hq = work.tile([P, width], U32, name="hq" + name, align_bytes=64)
            hz = work.tile([P, width], U8, name="hz" + name, align_bytes=64)
            nc.vector.quantize_mx(out=hq[:].bitcast(FP8X4), scales=hz[:], in_=ht[:])
            quantised[(n, halves)] = (hq, hz)

        def second_layer(n, halves, tag):
            e, chunk = UNITS[n]
            width = len(halves) * P
            hq, hz = quantised[(n, halves)]
            w2_words_e = w2[:, e, :].bitcast(FP4X4)
            w2_plane = s2[:, e * N : (e + 1) * N]
            acc = bank(tag, width)
            if chunk == 0:
                for i in halves:
                    nc.tensor.matmul_mx(
                        out=acc[:, i * N : (i + 1) * N],
                        lhsT=hq[:, i * P : (i + 1) * P].bitcast(FP8X4),
                        lhsT_scale=hz[:, i * P : (i + 1) * P],
                        rhs=w2_words_e,
                        rhs_scale=w2_plane,
                        start=True,
                        stop=True,
                    )
                ys = work.tile([P, C], F32, name="ys0")
                nc.scalar.copy(out=ys[:], in_=acc[:])
                shared_sums[chunk] = ys
                return
            nc.tensor.matmul_mx(
                out=acc[:],
                lhsT=w2_words_e,
                lhsT_scale=w2_plane,
                rhs=hq[:].bitcast(FP8X4),
                rhs_scale=hz[:],
                start=True,
                stop=True,
            )
            if e == SHARED:
                shared_sums[chunk] = acc
            else:
                c0 = e * C + halves[0] * P
                nc.scalar.copy(out=y[:, c0 : c0 + width], in_=acc[:])

        part_tags = ["part0", gelu_tag(LAST - 1, 1)] + [tag(LAST, j) for tag in (gelu_tag, hidden_tag) for j in BOTH]

        def part_tile(chunk, j):
            return work.tile([P, C], F32, name="part%d_%d" % (j, chunk), tag=part_tags[2 * chunk + j], align_bytes=64)

        def routed_results(chunk, j):
            return y[:].indirect(pos_sb[j][:, chunk * LIST_COLS : (chunk + 1) * LIST_COLS])

        def combine_turned(part_banks, total_bank):
            terms = [shared_sums[0]]
            for j in range(2):
                part = part_tile(0, j)
                nc.vector.tensor_copy(part[:], routed_results(0, j))
                part_turned = bank(part_banks[j], C)
                for i in range(2):
                    nc.tensor.transpose(part_turned[:, i * P : (i + 1) * P], part[:, i * P : (i + 1) * P], ident[:])
                scaled = work.tile([P, C], F32, name="scaled%d" % j)
                for i in range(2):
                    nc.scalar.activation(
                        out=scaled[:, i * P : (i + 1) * P],
                        in_=part_turned[:, i * P : (i + 1) * P],
                        func=COPY,
                        scale=gate_cols[:, 2 * j + i : 2 * j + i + 1],
                    )
                terms.append(scaled)
            total = bank(total_bank, C)
            for i in range(2):
                block = slice(i * P, (i + 1) * P)
                for m, term in enumerate(terms):
                    nc.tensor.matmul(
                        total[:, block], term[:, block], ident[:], start=(m == 0), stop=(m == len(terms) - 1), is_transpose=True
                    )
            result = work.tile([P, C], F32, name="result0")
            nc.scalar.copy(out=result[:], in_=total[:])
            nc.sync.dma_start(out=out[:, 0:C], in_=result[:])

        def combine(chunk):
            parts = []
            for j in range(2):
                part = part_tile(chunk, j)
                nc.vector.tensor_tensor(
                    out=part[:], in0=routed_results(chunk, j), in1=gate_sb[:, j, (chunk - 1) * C : chunk * C], op=MULT
                )
                parts.append(part)
            routed = work.tile([P, C], F32, name="routed%d" % chunk)
            nc.vector.tensor_tensor(out=routed[:], in0=parts[0][:], in1=parts[1][:], op=ADD)
            result = work.tile([P, C], F32, name="result%d" % chunk)
            nc.vector.tensor_tensor(out=result[:], in0=shared_sums[chunk][:], in1=routed[:], op=ADD)
            nc.sync.dma_start(out=out[:, chunk * C : (chunk + 1) * C], in_=result[:])

        held = [e for e, chunk in UNITS[3:5]] + [None] + [e for e, chunk in UNITS[5:7]]
        for n in range(LAST_ROUTED + 1):
            first_layer(n, 0)
            first_layer(n, 1)
            if n < len(held):
                if held[n] is None:
                    gather_scales(1, gelu_tag(n, 1))
                    late_loads()
                else:
                    gather_words(held[n], gelu_tag(n, 1))
            if n >= 1:
                turn_and_quantise(n - 1, BOTH, gelu_bank(n, 0))
            if n >= 2:
                second_layer(n - 2, BOTH, gelu_bank(n, 1))
        turn_and_quantise(LAST_ROUTED, (0,), "spare")
        turn_and_quantise(LAST_ROUTED, (1,), "sums")
        second_layer(LAST_ROUTED - 1, BOTH, "sums")
        second_layer(LAST_ROUTED, (0,), "sums")
        second_layer(LAST_ROUTED, (1,), "spare")
        for n in (LAST - 1, LAST):
            first_layer(n, 0)
            first_layer(n, 1)
        for j in BOTH:
            turn_and_quantise(LAST - 1 + j, BOTH, gelu_bank(LAST, j))
        for n in (LAST - 1, LAST):
            second_layer(n, BOTH, "sums")
        combine_turned(("spare", gelu_bank(LAST - 1, 1)), "spare")
        for chunk in range(1, CHUNKS):
            combine(chunk)
